import numpy as np, ml_dtypes
CORES = [3,7,11,15,131,135,139,143]
N = 8
BF = ml_dtypes.bfloat16
def gentries(a):
    return np.ascontiguousarray(a.reshape(8, 16, -1).transpose(0, 2, 1)).reshape(8, -1)
def gtable(e):
    e = np.asarray(e); return np.ascontiguousarray(e.reshape(8, -1, 16).transpose(0, 2, 1)).reshape(128, -1).astype(np.int32)
V, G, B, L, RO = 1024, 256, 3, 64, 3
W = V + B * G
def numbers(rng, ghost):
    s = (N, 8, V, 16)
    return np.where(rng.random(s) < ghost, rng.integers(V, W, s), rng.integers(0, V, s))
def image(t, nb):
    tw = np.concatenate([t, np.broadcast_to(np.arange(V, W), (N, 8, W - V))], axis=2)
    e = np.take_along_axis(tw, nb.reshape(N, 8, -1), 2).reshape(nb.shape)
    return np.take_along_axis(e, np.argsort(t, axis=-1)[..., None], 2)
def parts(rng, z, wild, mix):
    t = np.argsort(rng.random((N, 8, V)), axis=-1); nb = numbers(rng, 0.125)
    nz = np.where(rng.random(nb.shape) < wild, numbers(rng, 0.125), image(t, nb))
    x = np.clip(np.take_along_axis(z, t[:, :, None, :], 3) + rng.integers(-2, 3, z.shape), 0, 255)
    x = np.where(rng.random(z.shape) < 0.1, rng.integers(0, 256, z.shape), x)
    o = np.argsort(rng.random((N, 8, V)), axis=-1); m = t.copy()
    for r in range(N):
        for g in range(8):
            j = o[r, g, :int(V * mix[r, g])]; m[r, g, j] = t[r, g, np.roll(j, 1)]
    bx = np.ascontiguousarray(np.argsort(rng.random((N, 8, V)), axis=-1)[..., :G]); bz = np.take_along_axis(t, bx, 2)
    return {"x": x, "z": z, "nb": nb, "nz": nz, "m": m, "bx": bx, "bz": bz}
def pack(d):
    return {"x": np.ascontiguousarray(d["x"].reshape(N, 128, V)).astype(np.float32).astype(BF), "z": np.ascontiguousarray(d["z"].reshape(N, 128, V)).astype(np.float32).astype(BF),
            "nb": np.stack([gtable(a.reshape(8, -1)) for a in d["nb"]]), "nz": np.stack([gtable(a.reshape(8, -1)) for a in d["nz"]]),
            "m": d["m"].astype(np.int32), "im": np.argsort(d["m"], axis=-1).astype(np.int32),
            "bx": np.stack([gtable(a) for a in d["bx"]]), "bz": np.stack([gtable(a) for a in d["bz"]])}
def setup_inputs(rng):
    size = rng.permuted(np.tile(np.array([1, 1, 3, 3, 15, 63, 255, 255]), (N, 1)), axis=1)[:, :, None, None]
    z = rng.integers(0, size + 1, (N, 8, 16, V))
    wild = rng.choice(np.array([0.05, 0.2, 0.5, 1.0]), (N, 8, 1, 1)); mix = rng.choice(np.array([0.1, 0.3, 0.6, 1.0]), (N, 8))
    h = int(rng.integers(0, 8)); wild[:, h] = 0.0; mix[:, h] = 0.05
    return pack(parts(rng, z, wild, mix))
def setup_inputs_ties(rng):
    z = rng.integers(0, 2, (N, 8, 16, V)) * (rng.random((N, 8, 1, V)) < 0.5); z[:, 1, 1:] = 0
    d = parts(rng, z, rng.choice(np.array([0.2, 1.0]), (N, 8, 1, 1)), np.full((N, 8), 0.8))
    u = (np.arange(L) * (V // L))[1::2]
    for r in range(N):
        for g in (0, 2, 4, 6):
            s0 = np.flatnonzero(np.all(z[r, g] == 0, axis=0)); im = np.argsort(d["m"][r, g])
            d["nb"][r, g, u] = im[rng.choice(s0, (len(u), 16))]; d["nz"][r, g, d["m"][r, g, u]] = rng.choice(s0, (len(u), 16))
    d["nb"][:, 5] = rng.integers(0, V, (N, 1, 16))
    return pack(d)
def setup_inputs_crowd(rng):
    z = rng.integers(0, rng.choice(np.array([3, 15, 255]), (N, 8, 1, 1)) + 1, (N, 8, 16, V))
    d = parts(rng, z, np.ones((N, 8, 1, 1)), np.ones((N, 8)))
    for r in range(N):
        for g in range(8):
            n = (24, 160)[g % 2]
            s = np.concatenate([np.array([0, V - 1]), 1 + rng.permutation(V - 2)[:n - 2]]); e = np.concatenate([np.array([0, V - 1]), 1 + rng.permutation(V - 2)[:n - 2]])
            if g < 4: e = d["m"][r, g, s]
            ends = np.array([V, W - 1])
            d["nb"][r, g] = np.where(rng.random((V, 16)) < 0.05, rng.choice(ends, (V, 16)), rng.choice(s, (V, 16)))
            d["nz"][r, g] = np.where(rng.random((V, 16)) < 0.05, rng.choice(ends, (V, 16)), rng.choice(e, (V, 16)))
            d["bx"][r, g] = rng.choice(s, G); d["bz"][r, g] = rng.choice(e, G)
    return pack(d)
def setup_inputs_border(rng):
    z = rng.integers(0, rng.choice(np.array([3, 15, 255]), (N, 8, 1, 1)) + 1, (N, 8, 16, V))
    d = parts(rng, z, np.ones((N, 8, 1, 1)), np.ones((N, 8)))
    for r in range(N):
        for g in range(8):
            s = rng.permutation(V)[:160]; e = d["m"][r, g, s]
            d["nb"][r, g] = np.where(rng.random((V, 16)) < 0.3, rng.integers(V, W, (V, 16)), rng.choice(s, (V, 16)))
            d["nz"][r, g] = np.where(rng.random((V, 16)) < 0.3, rng.integers(V, W, (V, 16)), rng.choice(e, (V, 16)))
            d["bx"][r, g] = rng.choice(s, G); d["bz"][r, g] = rng.choice(e, G)
    d["bx"][:, :, 0] = 0; d["bx"][:, :, G - 1] = V - 1; d["bz"][:, :, 0] = V - 1; d["bz"][:, :, G - 1] = 0
    q = rng.permutation(8); d["nb"][:, q[0]] = rng.integers(V, W, (N, V, 16)); d["nz"][:, q[1]] = rng.integers(V, W, (N, V, 16))
    d["nb"][:, :, 0, :2] = np.array([V, W - 1])
    return pack(d)
def agree(d, r, g):
    t = np.concatenate([d["m"][r, g], np.arange(V, W)]); d["nz"][r, g, t[:V]] = t[d["nb"][r, g]]
def early(rng, d, r, g, n):
    st = np.arange(L) * (V // L); o = rng.permutation(np.setdiff1d(np.arange(V), np.concatenate([st, d["bx"][r, g]])))
    p = o[:2 * n]; a = d["nb"][r, g][st]; a[np.isin(a, p)] = o[2 * n]
    a[rng.permutation(L)[:n], rng.integers(0, 16, n)] = p[:n]; d["nb"][r, g, st] = a
    agree(d, r, g); t = d["m"][r, g].copy(); d["m"][r, g, p] = t[np.roll(p, n)]
def late(rng, d, r, g):
    st = np.arange(L) * (V // L); o = rng.permutation(np.setdiff1d(np.arange(V), np.concatenate([st, d["bx"][r, g], np.array([819, V - 1])])))
    p = o[:6].copy(); s = p[:3]; f = int(o[6]); b = o[7:7 + L].copy(); c = o[7 + L:7 + 2 * L].copy(); rest = o[7 + 2 * L:]
    j = 1 + rng.permutation(L - 1)[:3]; b[j[0]] = 819
    nb = d["nb"][r, g]; nb[np.isin(nb, p)] = f
    nb[p] = rng.choice(rest, (6, 16)); nb[s, rng.integers(0, 16, 3)] = f
    nb[st, 0] = b; nb[b, 0] = c; nb[819, 0] = rng.integers(V, W)
    nb[np.array([b[j[1]], c[j[2]], V - 1]), rng.integers(1, 16, 3)] = s
    agree(d, r, g); t = d["m"][r, g].copy(); z = d["z"][r, g]
    z[:] = rng.integers(0, 200, (16, 1)); z[:, t[s]] += rng.integers(1, 5, (16, 3)); z[int(rng.integers(0, 16)), t[f]] += rng.integers(1, 16)
    d["m"][r, g, p] = t[np.roll(p, 3)]
def setup_inputs_still(rng):
    z = rng.integers(0, 256, (N, 8, 16, V)); d = parts(rng, z, np.zeros((N, 8, 1, 1)), np.zeros((N, 8)))
    q, q2, q3 = [int(i) for i in rng.permutation(N)[:3]]; h, h2 = [int(i) for i in rng.permutation(8)[:2]]; st = np.arange(L) * (V // L)
    room = [L] + [(287 - L + i) // 5 for i in range(5)]
    for r in range(N):
        for g in range(8):
            if r == q or g == h: continue
            if r in (q2, q3):
                if g == h2: late(rng, d, r, g)
                elif r == q3: early(rng, d, r, g, room.pop())
                continue
            c = np.unique(d["nb"][r, g, st]); c = np.setdiff1d(c[c < V], np.concatenate([st, d["bx"][r, g]]))
            p = rng.permutation(c)[:2 * int(rng.integers(1, 4))]
            d["m"][r, g, p] = d["m"][r, g, p.reshape(-1, 2)[:, ::-1].reshape(-1)]
    return pack(d)
def setup_inputs_spread(rng):
    z = (np.exp2(8 * rng.random((N, 8, 1, V))) * rng.random((N, 8, 16, V)) * (rng.random((N, 8, 1, V)) > 0.0625)).astype(np.int64)
    wild = rng.choice(np.array([0.05, 0.3, 1.0]), (N, 8, 1, 1)); mix = rng.choice(np.array([0.2, 0.5, 1.0]), (N, 8))
    for h in rng.permutation(8)[:2]:
        u = rng.integers(0, 4, (N, 16, V)); z[:, h] = np.where(rng.random((N, 1, V)) < 0.5, u, 255 - u); wild[:, h] = 1.0; mix[:, h] = 1.0
    return pack(parts(rng, z, wild, mix))
def check_inputs(d):
    bad = []
    for k in ("x", "z"):
        a = np.asarray(d[k]).astype(np.float32)
        if not np.all((a >= 0) & (a <= 255) & (a == np.floor(a))): bad.append("whole numbers 0 to 255 in " + k)
    for k, hi in (("nb", W - 1), ("nz", W - 1), ("m", V - 1), ("im", V - 1), ("bx", V - 1), ("bz", V - 1)):
        if np.min(d[k]) < 0 or np.max(d[k]) > hi: bad.append("range of " + k)
    if not np.all(np.sort(d["m"], axis=-1) == np.arange(V)): bad.append("m is a bijection")
    elif not np.all(np.argsort(d["m"], axis=-1) == d["im"]): bad.append("im is the inverse of m")
    return bad
def reference(x, z, nb, nz, m, im, bx, bz):
    X = x.astype(np.float32).astype(np.int64).reshape(N, 8, 16, V); Z = z.astype(np.float32).astype(np.int64).reshape(N, 8, 16, V)
    nv = np.stack([gentries(a) for a in nb]).astype(np.int64).reshape(N, 8, V, 16); ns = np.stack([gentries(a) for a in nz]).astype(np.int64).reshape(N, 8, V, 16)
    M = m.astype(np.int64); I = im.astype(np.int64)
    b1 = np.stack([gentries(a) for a in bx]).astype(np.int64); b2 = np.stack([gentries(a) for a in bz]).astype(np.int64)
    lane = np.arange(L); v = np.tile(lane * (V // L), (N, 8, 1)); last = np.zeros(N, np.int64)
    for rnd in range(RO):
        Y = np.take_along_axis(Z, M[:, :, None, :], 3)
        ey = np.take_along_axis(Y, b1[:, :, None, :], 3); ez = np.take_along_axis(Z, b2[:, :, None, :], 3)
        YW = np.concatenate([Y] + [np.roll(ey, -d, axis=0) for d in range(1, B + 1)], axis=3)
        ZW = np.concatenate([Z] + [np.roll(ez, -d, axis=0) for d in range(1, B + 1)], axis=3)
        th = last & 31; last = np.zeros(N, np.int64)
        for r in range(N):
            for g in range(8):
                Yg, Zg, n1, n2, at = YW[r, g], ZW[r, g], nv[r, g], ns[r, g], v[r, g].copy()
                na = n1[at]; nq = n2[M[r, g, at]]
                D = np.add.reduce(np.abs(Yg[:, na] - Zg[:, nq]), axis=0); k = np.argmax(D, axis=1)
                a = na[lane, k]; q = nq[lane, k]; live = (D[lane, k] > 0) & (a < V) & (q < V)
                ac = np.minimum(a, V - 1); qc = np.minimum(q, V - 1); w = I[r, g, qc]; p = M[r, g, ac]
                Aa = Yg[:, n1[ac]]; Aw = Yg[:, n1[w]]; Ba = Zg[:, n2[p]]; Bw = Zg[:, n2[qc]]
                gain = np.add.reduce(np.abs(Aa - Ba) + np.abs(Aw - Bw) - np.abs(Aa - Bw) - np.abs(Aw - Ba), axis=(0, 2))
                prop = live & (gain > th[r])
                first = np.full(V, L); np.minimum.at(first, ac[prop], lane[prop]); np.minimum.at(first, w[prop], lane[prop])
                com = prop & (first[ac] >= lane) & (first[w] >= lane)
                last[r] += np.count_nonzero(com)
                v[r, g] = np.where(com, a, np.where(q < V, w, (5 * at + 1) & (V - 1)))
                a, w, p, q = a[com], w[com], p[com], q[com]
                M[r, g, a] = q; M[r, g, w] = p; I[r, g, q] = a; I[r, g, p] = w
                for vert, site in ((a, q), (w, p)):
                    old = Z[r, g][:, site]; Z[r, g][:, site] = old + np.clip(X[r, g][:, vert] - old, -1, 1)
    return {"mo": M.astype(np.float32), "zo": Z.reshape(N, 128, V).astype(np.float32).astype(BF)}

@@ -1,0 +1,441 @@
+from concourse.bass import DstId, RemoteDMATransfer
+from concourse.mybir import AluOpType as O, AxisListType, ActivationFunctionType as AF
+
+F4, B2, I4, U2 = "float32", "bfloat16", "int32", "uint16"
+_W = {
+    B2: dict(ZW=1920, YW=1920, tX=1024, SY=512 + 256, SZ=768, Yt=1024, Zt=1024, ng=256, AD=1024, At=1024, Bt=1024, Bp=1024, T1=1024,
+             T2=1024, R1=1024, R2=1024, zz=128, xx=128, cl=128, nzv=128, EQ=640, gh=128, kz2=64, npr=64, WT=512, cnt=2,
+             identb=128, identn=128, biasd=128, blkp=128, blkm=128, blkV=128, idV=128, idN=128, Es=144, W4=512, ones64=64,
+             onesb=128),
+    F4: dict(MF=1152, mlf=256, nf=128, KT=64, Fs=64, OHt=64, OH=64, pr=128, mk=128, sc=128, WP=128, AQ=128, NR=128, mk2=128,
+             sc2=128, NLc=16, NLd=16, kz=64, TH=64, x1=64, sp=64, cm=64, cl2=64, VL=4, V5=4, oq=4, d1=4, d2=4, alt=4, da=4,
+             d3=4, cn=2, thc=2, onesf=128, b1=128, blkf=128, ff=2, f15=2, itf=128, mask=128, reset=128, identf=128, q25=16,
+             s0=16, pwr=16, pm=16, pwc=2, c25=64, c00=64, thr=64, t1=64, mm1=64, thrM=64, nmB=64, c16f=4, lane4=4, lm16=16),
+    I4: dict(tNB=1024, tNZ=1024, tNZM=1152, tNBI=1152, tM=1152, tIM=1152, ml=256, bl=32, v5a=4, v5b=4, thi=2, thj=2, c_it=128,
+             c_p=2, c_c16=4, fI=2),
+    U2: dict(ML=128, BL=32, L1=128, LAQ=8, L2=256, LWP=8, OFF=16, vl=4),
+}
+SCRATCH = {n: ("sbuf", [128, w], d) for d in _W for n, w in _W[d].items()}
+for _i in range(8):
+    SCRATCH["pb%d" % _i] = ("psum", [128, 512], F4)
+SEMAPHORES = ["cv", "cs", "cp", "cg", "ld_z", "ld_b", "ld_m", "ld_im", "ld_nz", "ld_nb", "ld_x", "ld_M", "ld_IM", "st_z", "st_m",
+              "aY0", "aY1", "aY2", "aZ0", "aZ1", "aZ2", "rdy1", "rdy2", "sl"]
+N = 8
+OWN = 128
+CH = [(0, 16), (16, 40), (40, 64)]
+
+
+def rank_program(g, core, T, topo):
+    rank = T.rank_of(core)
+    if rank is None:
+        return
+    QUEUE = {"V": g.vector, "S": g.scalar, "P": g.tensor, "G": g, "Y": g.sync}
+    SEM = {"V": "cv", "S": "cs", "P": "cp", "G": "cg"}
+    cnt = {"cv": 0, "cs": 0, "cp": 0, "cg": 0}
+    total = {}
+    seen = {q: {} for q in QUEUE}
+    acc = {}
+
+    def need(q, sem, val):
+        if seen[q].get(sem, 0) < val:
+            QUEUE[q].wait_ge(T.sem[sem], val)
+            seen[q][sem] = val
+
+    def order(q, reads, writes):
+        w = {}
+        for kind, regs in (("r", reads), ("w", writes)):
+            for (n, a, b) in regs:
+                ps = n[:2] == "pb"
+                for (a2, b2, k2, q2, s2, v2) in acc.get(n, ()):
+                    if ps:
+                        if q2 == q and (q == "P" or (kind == "r" and k2 == "r")):
+                            continue
+                    else:
+                        if (kind == "r" and k2 == "r") or b2 <= a or b <= a2:
+                            continue
+                    w[s2] = max(w.get(s2, 0), v2)
+        for s, v in w.items():
+            need(q, s, v)
+
+    def record(q, reads, writes, sem, val):
+        for kind, regs in (("r", reads), ("w", writes)):
+            for (n, a, b) in regs:
+                l = [e for e in acc.get(n, []) if not (e[0] == a and e[1] == b and e[2] == kind and e[3] == q)]
+                l.append((a, b, kind, q, sem, val))
+                acc[n] = l
+
+    def emit(q, calls, outs, ins):
+        reads = [r for i in ins for r in i[1] + i[2]] + [r for o in outs for r in o[2]]
+        writes = [r for o in outs for r in o[1]]
+        order(q, reads, writes)
+        for c in calls:
+            last = c()
+        s = SEM[q]
+        cnt[s] += 1
+        last.then_inc(T.sem[s], 1)
+        record(q, reads, writes, s, cnt[s])
+
+    def R(n, a, b, s=1):
+        return (T[n][:, a:b] if s == 1 else T[n][:, a:b:s], [(n, a, b)], [])
+
+    def C(n, c=0):
+        return R(n, c, c + 1)
+
+    def IND(n, a, b, off):
+        return (T[n][:, a:b].indirect(off[0]), [(n, a, b)], off[1])
+
+    def tup(*xs):
+        return [x for x in xs if isinstance(x, tuple)]
+
+    def raw(x):
+        return x[0] if isinstance(x, tuple) else x
+
+    def vcopy(o, i):
+        emit("V", [lambda: g.vector.tensor_copy(out=o[0], in_=i[0])], [o], [i])
+
+    def vtt(o, a, b, op):
+        emit("V", [lambda: g.vector.tensor_tensor(out=o[0], in0=a[0], in1=b[0], op=op)], [o], [a, b])
+
+    def vts(o, a, s1, s2, op0, op1=None):
+        if op1 is None:
+            f = lambda: g.vector.tensor_scalar(out=o[0], in0=a[0], scalar1=raw(s1), scalar2=None, op0=op0)
+        else:
+            f = lambda: g.vector.tensor_scalar(out=o[0], in0=a[0], scalar1=raw(s1), scalar2=raw(s2), op0=op0, op1=op1)
+        emit("V", [f], [o], [a] + tup(s1, s2))
+
+    def vscan(o, d0, d1, init, op0, op1):
+        emit("V", [lambda: g.vector.tensor_tensor_scan(out=o[0], data0=d0[0], data1=d1[0], initial=init, op0=op0, op1=op1)],
+             [o], [d0, d1])
+
+    def vset(o, c):
+        emit("V", [lambda: g.vector.memset(o[0], c)], [o], [])
+
+    def vtr(o, i):
+        emit("V", [lambda: g.vector.transpose(out=o[0], in_=i[0])], [o], [i])
+
+    def vsum(o, i):
+        emit("V", [lambda: g.vector.tensor_reduce(out=o[0], in_=i[0], axis=AxisListType.X, op=O.add)], [o], [i])
+
+    def sact(o, i, func=AF.Copy, scale=1.0):
+        emit("S", [lambda: g.scalar.activation(out=o[0], in_=i[0], func=func, scale=raw(scale))], [o], [i] + tup(scale))
+
+    def mm(o, l, r, st, sp):
+        return (lambda: g.tensor.matmul(o[0], l[0], r[0], st, sp)), o, l, r
+
+    def pe(ms):
+        emit("P", [m[0] for m in ms], [m[1] for m in ms], [x for m in ms for x in (m[2], m[3])])
+
+    def load(q, sem, n, o, in_ap, tot):
+        order(q, [], o[1])
+        QUEUE[q].dma_start(out=o[0], in_=in_ap).then_inc(T.sem[sem], 16)
+        total[sem] = 16 * tot
+        record("D" + sem, [], o[1], sem, 16 * tot)
+
+    def store(q, sem, out_ap, i):
+        order(q, i[1], [])
+        QUEUE[q].dma_start(out=out_ap, in_=i[0]).then_inc(T.sem[sem], 16)
+        total[sem] = 16
+
+    load("S", "ld_z", 0, R("ZW", OWN, OWN + 1024), T.z[:], 1)
+    load("S", "ld_b", 0, R("bl", 0, 16), T.bx[:], 2)
+    load("S", "ld_b", 0, R("bl", 16, 32), T.bz[:], 2)
+    load("S", "ld_nz", 0, R("tNZ", 0, 1024), T.nz[:], 1)
+    load("S", "ld_nb", 0, R("tNB", 0, 1024), T.nb[:], 1)
+    for k in range(8):
+        load("Y", "ld_m", 0, (T.ml[0:64, 16 * k:16 * k + 16], [("ml", 16 * k, 16 * k + 16)], []), T.m[k:k + 1, :], 8)
+    for k in range(8):
+        load("Y", "ld_im", 0, (T.ml[0:64, 128 + 16 * k:144 + 16 * k], [("ml", 128 + 16 * k, 144 + 16 * k)], []), T.im[k:k + 1, :], 8)
+    for f in range(16):
+        load("Y", "ld_IM", 0, (T.tIM[f:128:16, OWN:OWN + 1024], [("tIM", OWN, OWN + 1024)], []), T.im[:], 16) if False else None
+    load("Y", "ld_x", 0, R("tX", 0, 1024), T.x[:], 1)
+
+    def spread(sem, n, src):
+        order("Y", [], [(n, OWN, OWN + 1024)])
+        for f in range(16):
+            g.sync.dma_start(out=T[n][f:128:16, OWN:OWN + 1024], in_=src[:]).then_inc(T.sem[sem], 16)
+        total[sem] = 256
+        record("D" + sem, [], [(n, OWN, OWN + 1024)], sem, 256)
+    spread("ld_IM", "tIM", T.im)
+    spread("ld_M", "tM", T.m)
+
+    def giota(o, pat, ch):
+        emit("G", [lambda: g.iota(o[0], pat, 0, ch)], [o], [])
+
+    def gsel(o, i, pat, base, ch):
+        emit("G", [lambda: g.affine_select(o[0], i[0], pat, O.is_ge, 0.0, base, ch)], [o], [i])
+    a128 = lambda n: R(n, 0, 128)
+    a64 = lambda n: R(n, 0, 64)
+    vset(a128("onesf"), 1.0)
+    giota(R("c_p", 0, 2), [[0, 2]], 1)
+    giota(a128("c_it"), [[0, 8], [1, 16]], 0)
+    gsel(a128("b1"), a128("onesf"), [[-16, 8], [0, 16]], 0, 1)
+    gsel(a128("blkf"), a128("b1"), [[16, 8], [0, 16]], 15, -1)
+    giota(R("c_c16", 0, 4), [[16, 4]], 0)
+    vts(R("fI", 0, 2), R("c_p", 0, 2), 15, None, O.bitwise_and)
+    vcopy(R("ff", 0, 2), R("fI", 0, 2))
+    vcopy(a128("itf"), a128("c_it"))
+    vts(a128("mask"), a128("itf"), C("ff"), None, O.is_equal)
+    vts(a128("reset"), a128("itf"), 0.0, None, O.is_gt)
+    vtt(a128("identf"), a128("blkf"), a128("mask"), O.mult)
+
+    peers_to = [T.cores[(rank - d) % N] for d in (1, 2, 3)]
+    peers_from = [T.cores[(rank + d) % N] for d in (1, 2, 3)]
+    emask = 0xFFFF
+    for d in peers_to:
+        emask &= topo.mask(core, d)
+    neng = bin(emask).count("1")
+    nsl = [0]
+    allsem = {}
+
+    def send(e, n, win):
+        i = R(n, 256 * e, 256 * e + 256)
+        order("G", i[1], [])
+        ids, dsts = [], []
+        for d in (1, 2, 3):
+            rid, pid = topo.addr(peers_to[d - 1], core)
+            ids.append(DstId(rid=rid, pnc=pid))
+            c = OWN + 1024 + 256 * (d - 1)
+            dsts.append(T[win][:, c:c + 256])
+        s = "a%s%d" % (win[0], e)
+        g.remote_dma_fused([RemoteDMATransfer(dst_ids=ids, dma_engine_mask=emask, remote_sem=T.sem[s], srcs=[i[0]], dsts=dsts)],
+                           local_sem=T.sem.sl)
+        nsl[0] += neng
+        total[s] = 3 * neng
+        record("A", [], [(win, OWN + 1024, OWN + 1792)], s, 3 * neng)
+
+    Zown, Zall = ("ZW", OWN, OWN + 1024), ("ZW", OWN, OWN + 1792)
+    Yown, Yall = ("YW", OWN, OWN + 1024), ("YW", OWN, OWN + 1792)
+
+    vcopy(R("BL", 0, 32), R("bl", 0, 32))
+    sact(R("SZ", 0, 256), IND(*Zown, R("BL", 16, 32)))
+    mlp = lambda n, a: (T[n][0:64, a:a + 128], [(n, a, a + 128)], [])
+    id64 = (T.identf[0:64, 0:64], [("identf", 0, 128)], [])
+
+    def mlist(a, bank):
+        vcopy(mlp("mlf", a), mlp("ml", a))
+        o, i = R(bank, 0, 64), mlp("mlf", a)
+        emit("P", [lambda: g.tensor.transpose(o[0], i[0], id64[0])], [o], [i, id64])
+        vcopy(R("ML", a // 2, a // 2 + 64), o)
+    mlist(0, "pb0")
+    vcopy(R("YW", OWN, OWN + 512), IND(*Zown, R("ML", 0, 32)))
+    sact(R("YW", OWN + 512, OWN + 1024), IND(*Zown, R("ML", 32, 64)))
+    vcopy(R("SY", 0, 256), IND(*Yown, R("BL", 0, 16)))
+    send(0, "SZ", "ZW")
+    send(0, "SY", "YW")
+    vts(a128("identn"), a128("identf"), -1.0, None, O.mult)
+    vcopy(a128("identb"), a128("identf"))
+    vcopy(R("tNZM", OWN, OWN + 1024), IND("tNZ", 0, 1024, R("ML", 0, 64)))
+    mlist(128, "pb1")
+    vcopy(R("L1", 64, 128), R("tNZM", OWN, OWN + 1024, 16))
+    vcopy(R("L1", 0, 64), R("tNB", 0, 1024, 16))
+    vts(C("f15"), C("ff"), -1.0, 15.0, O.mult, O.add)
+    vts(a128("biasd"), a128("identf"), C("f15"), None, O.mult)
+    vset(a64("ones64"), 1.0)
+    vset(R("Es", 0, 144), 0.0)
+    vts(R("Es", 15, 143, 16), R("blkf", 0, 128, 16), 16.0, None, O.mult)
+    vcopy(R("tNBI", OWN, OWN + 1024), IND("tNB", 0, 1024, R("ML", 64, 128)))
+    sact(a128("blkp"), a128("blkf"), AF.Copy, 2.0)
+    sact(a128("blkm"), a128("blkf"), AF.Copy, -2.0)
+    sact(a128("blkV"), a128("blkf"), AF.Copy, -float(2 ** 20))
+    sact(a128("idV"), a128("identf"), AF.Copy, -float(2 ** 20))
+    sact(a128("idN"), a128("identf"), AF.Copy, float(2 ** 70))
+    sact(a128("onesb"), a128("onesf"))
+    vts(R("q25", 0, 16), R("reset", 0, 16), 0.25, None, O.mult)
+    vts(R("s0", 0, 16), R("reset", 0, 16), -1.0, 1.0, O.mult, O.add)
+    vset(a64("c25"), 0.25)
+    vset(a64("c00"), 0.0)
+    vscan(R("pwr", 0, 16), R("q25", 0, 16), R("s0", 0, 16), 0.0, O.mult, O.add)
+    vscan(a64("thr"), a64("c25"), a64("c00"), 3.0 * 4.0 ** 33, O.mult, O.add)
+    vtt(R("pm", 0, 16), R("pwr", 0, 16), R("mask", 0, 16), O.mult)
+    vts(a64("mm1"), a64("mask"), -1.0, None, O.add)
+    vsum(C("pwc"), R("pm", 0, 16))
+    vtt(a64("t1"), a64("thr"), a64("mask"), O.mult)
+    vts(a64("nmB"), a64("mask"), -float(2 ** 24), float(2 ** 24), O.mult, O.add)
+    for c in range(4):
+        vts(R("W4", 128 * c, 128 * c + 128), a128("blkf"), C("pwc"), 4.0 ** (32 - 16 * c), O.mult, O.mult)
+    vtt(a64("thrM"), a64("t1"), a64("mm1"), O.add)
+    vcopy(R("c16f", 0, 4), R("c_c16", 0, 4))
+    vts(R("lane4", 0, 4), R("c16f", 0, 4), C("ff"), None, O.add)
+    for n in range(4):
+        vts(R("lm16", 4 * n, 4 * n + 4), R("lane4", 0, 4), -float(OWN), None, O.add)
+    vts(R("VL", 0, 4), R("lane4", 0, 4), 16.0, None, O.mult)
+
+    def step_lists():
+        vcopy(a128("nf"), a128("L1"))
+        vts(R("v5a", 0, 4), R("VL", 0, 4), 5.0, 1.0, O.mult, O.add)
+        vts(R("v5b", 0, 4), R("v5a", 0, 4), 1023, None, O.bitwise_and)
+        vcopy(R("V5", 0, 4), R("v5b", 0, 4))
+    step_lists()
+
+    for r in range(3):
+        mt = "tM" if r == 0 else "MF"
+        more = r < 2
+        for j, (a, b) in enumerate(CH):
+            vcopy(R("Yt", 16 * a, 16 * b), IND(*Yall, R("L1", a, b)))
+            sact(R("Zt", 16 * a, 16 * b), IND(*Zall, R("L1", 64 + a, 64 + b)))
+            o = R("pb%d" % j, 0, 16 * (b - a))
+            pe([mm(o, a128("identb"), R("Yt", 16 * a, 16 * b), True, False),
+                mm(o, a128("identn"), R("Zt", 16 * a, 16 * b), False, True)])
+        vts(R("ng", 0, 256), R("pb0", 0, 256), -1.0, None, O.mult)
+        vtt(R("AD", 0, 256), R("pb0", 0, 256), R("ng", 0, 256), O.max)
+        for j in (1, 2):
+            a, b = CH[j]
+            sact(R("AD", 16 * a, 16 * b), R("pb%d" % j, 0, 16 * (b - a)), AF.Abs)
+        K = R("pb3", 0, 64)
+        pe([mm(K, a128("biasd"), a64("ones64"), True, False)] +
+           [mm(K, R("Es", 15 - k, 143 - k), R("AD", k, 1024, 16), False, k == 15) for k in range(16)])
+        vtr(a64("KT"), K)
+        vscan(a64("Fs"), a64("reset"), a64("KT"), 0.0, O.mult, O.max)
+        for s in range(4):
+            vts(R("OHt", 16 * s, 16 * s + 16), R("KT", 16 * s, 16 * s + 16), C("Fs", 16 * s + 15), None, O.is_equal)
+        vtr(a64("OH"), a64("OHt"))
+        vtt(R("pr", 0, 64), a64("OH"), R("nf", 0, 64), O.mult)
+        vtt(R("pr", 64, 128), a64("OH"), R("nf", 64, 128), O.mult)
+        ROW = R("pb4", 0, 128)
+        pe([mm(ROW, a128("blkf"), a128("pr"), True, True)])
+        vtt(a128("mk"), ROW, a128("mask"), O.mult)
+        vscan(a128("sc"), a128("reset"), a128("mk"), 0.0, O.mult, O.add)
+        vts(R("LAQ", 0, 8), R("sc", 15, 128, 16), 1023.0, None, O.min)
+        la, lq = R("LAQ", 0, 4), R("LAQ", 4, 8)
+        vcopy(R("L2", 0, 64), IND("tNZM", OWN, OWN + 1024, la))
+        for h in (0, 1):
+            sact(R("Bt", 512 * h, 512 * h + 512), IND(*Zall, R("L2", 32 * h, 32 * h + 32)))
+        vcopy(R("L2", 64, 128), IND("tNBI", OWN, OWN + 1024, lq))
+        sact(R("At", 512, 1024), IND(*Yall, R("L2", 96, 128)))
+        vcopy(R("L2", 128, 192), IND("tNZ", 0, 1024, lq))
+        for h in (0, 1):
+            sact(R("Bp", 512 * h, 512 * h + 512), IND(*Zall, R("L2", 128 + 32 * h, 160 + 32 * h)))
+        vcopy(R("At", 0, 512), IND(*Yall, R("L2", 64, 96)))
+        vcopy(R("L2", 192, 256), IND("tNB", 0, 1024, la))
+        vcopy(R("WP", 0, 64), IND("tIM", OWN, OWN + 1024, lq))
+        vcopy(R("WP", 64, 128), IND(mt, OWN, OWN + 1024, la))
+        vts(a128("gh"), ROW, 1024.0, None, O.is_ge)
+        vts(a64("kz"), K, 16.0, None, O.is_lt)
+        vtt(a64("kz2"), a64("kz"), a64("OH"), O.mult)
+        dif = []
+        for j, (bk, src, h) in enumerate([("pb0", "Bt", 0), ("pb1", "Bt", 1), ("pb2", "Bp", 0), ("pb5", "Bp", 1)]):
+            s = slice(512 * h, 512 * h + 512)
+            o = R(bk, 0, 512)
+            pe([mm(o, a128("identb"), R(src, s.start, s.stop), True, False),
+                mm(o, a128("identn"), R("At", s.start, s.stop), False, True)])
+            dif.append(o)
+        sact(a128("AQ"), ROW)
+        sact(R("NR", 0, 128, 2), R("AQ", 0, 64))
+        sact(R("NR", 1, 128, 2), R("WP", 0, 64))
+        for h in (0, 1):
+            sact(R("R1", 512 * h, 512 * h + 512), dif[h], AF.Relu)
+        for h in (0, 1):
+            sact(R("R2", 512 * h, 512 * h + 512), dif[2 + h], AF.Relu)
+        vtt(a128("mk2"), a128("WP"), a128("mask"), O.mult)
+        vtt(R("T1", 0, 1024), IND(*Yall, R("L2", 192, 256)), R("Bt", 0, 1024), O.max)
+        vscan(a128("sc2"), a128("reset"), a128("mk2"), 0.0, O.mult, O.add)
+        vts(R("NLc", 0, 8), R("sc", 15, 128, 16), 1023.0, None, O.min)
+        vcopy(R("NLc", 8, 16), R("sc2", 15, 128, 16))
+        vcopy(R("LWP", 0, 8), R("sc2", 15, 128, 16))
+        vtt(R("T2", 0, 1024), IND(*Yall, R("L2", 192, 256)), R("Bp", 0, 1024), O.max)
+        if more:
+            need("G", "cv", cnt["cv"])
+            need("G", "cs", max(e[5] for w in ("ZW", "YW") for e in acc[w] if e[3] == "S"))
+            for d in peers_from:
+                rid, pid = topo.addr(d, core)
+                g.remote_sem_update(T.sem["rdy%d" % (r + 1)], T.sem.sl, pid, rid, 1 << topo.engines(core, d)[0])
+                nsl[0] += 1
+            total["rdy%d" % (r + 1)] = 3
+        sact(R("zz", 0, 64), IND(*Zown, lq))
+        sact(R("xx", 0, 64), IND("tX", 0, 1024, la))
+        sact(R("zz", 64, 128), IND(*Zown, R("LWP", 4, 8)))
+        sact(R("xx", 64, 128), IND("tX", 0, 1024, R("LWP", 0, 4)))
+        eqs, at = [], 0
+        for c in range(4):
+            for col in (C("sc", 16 * c + 15), C("sc2", 16 * c + 15)):
+                w = 128 - 32 * c
+                vts(R("EQ", at, at + w), R("NR", 32 * c, 128), col, None, O.is_equal)
+                eqs.append((c, at, w))
+                at += w
+        vtt(R("NLd", 0, 16), R("NLc", 0, 16), R("lm16", 0, 16), O.subtract)
+        if more:
+            vts(R("oq", 0, 4), R("sc", 79, 128, 16), 1024.0, None, O.is_lt)
+            vtt(R("d1", 0, 4), R("sc2", 15, 64, 16), R("V5", 0, 4), O.subtract)
+            vtt(R("d2", 0, 4), R("d1", 0, 4), R("oq", 0, 4), O.mult)
+            vtt(R("alt", 0, 4), R("d2", 0, 4), R("V5", 0, 4), O.add)
+            vtt(R("da", 0, 4), R("sc", 15, 64, 16), R("alt", 0, 4), O.subtract)
+        Gn = R("pb6", 0, 64)
+        pe([mm(Gn, a128("idV"), R("gh", 0, 64), True, False), mm(Gn, a128("idV"), R("gh", 64, 128), False, False),
+            mm(Gn, a128("blkV"), a64("kz2"), False, False)])
+        for n, l in (("T1", "blkp"), ("R1", "blkm"), ("T2", "blkm"), ("R2", "blkp")):
+            pe([mm(Gn, a128(l), R(n, k, 1024, 16), False, n == "R2" and k == 15) for k in range(16)])
+        if r:
+            vtt(a64("x1"), Gn, a64("TH"), O.is_gt)
+            vts(a64("npr"), Gn, C("thc"), None, O.is_le)
+        else:
+            vtt(a64("x1"), Gn, a64("nmB"), O.is_gt)
+            vts(a64("npr"), Gn, 0.0, None, O.is_le)
+        vscan(a64("sp"), a64("reset"), a64("x1"), 0.0, O.mult, O.add)
+        for c in (0, 1):
+            vts(R("WT", 128 * c, 128 * c + 128), R("W4", 128 * c, 128 * c + 128), C("sp", 16 * c + 15), None, O.mult)
+        for c in (2, 3):
+            sact(R("WT", 128 * c, 128 * c + 128), R("W4", 128 * c, 128 * c + 128), AF.Copy, C("sp", 16 * c + 15))
+        xz = R("pb4", 128, 256)
+        pe([mm(xz, a128("identb"), a128("xx"), True, False), mm(xz, a128("identn"), a128("zz"), False, True)])
+        vts(a128("cl"), xz, -1.0, 1.0, O.max, O.min)
+        CS = R("pb7", 0, 64)
+        ms = [mm(CS, a128("idN"), a64("npr"), True, False)]
+        for (c, at, w) in eqs[::-1]:
+            for nm in (0, 1):
+                ms.append([R("pb7", 16 * c, 64), R("WT", 128 * c, 128 * c + 128), R("EQ", at + nm, at + w, 2)])
+        ms = ms[:1] + [mm(o, l, x, False, i == len(ms) - 2) for i, (o, l, x) in enumerate(ms[1:])]
+        pe(ms)
+        nzp = R("pb3", 128, 256)
+        pe([mm(nzp, a128("identb"), a128("zz"), True, False), mm(nzp, a128("identb"), a128("cl"), False, True)])
+        sact(a128("nzv"), nzp)
+        vtt(a64("cm"), CS, a64("thrM"), O.is_le)
+        vscan(a64("cl2"), a64("reset"), a64("cm"), 0.0, O.mult, O.add)
+        for c in range(4):
+            vts(R("OFF", c, 16, 4), R("NLd", c, 16, 4), C("cl2", 16 * c + 15), C("lane4", c), O.mult, O.add)
+        oa, oqq, ow, op = [R("OFF", 4 * n, 4 * n + 4) for n in range(4)]
+        sca = lambda n, off, d: vcopy(IND(n, 0, OWN + 1024, off), d)
+        sca("ZW", oqq, R("nzv", 0, 64))
+        sca("ZW", op, R("nzv", 64, 128))
+        if not more:
+            store("Y", "st_z", T.zo[:], R("ZW", OWN, OWN + 1024))
+            sca("MF", oa, R("AQ", 64, 128))
+            sca("MF", ow, R("WP", 64, 128))
+            store("Y", "st_m", T.mo[:], (T.MF[0:128:16, OWN:OWN + 1024], [("MF", OWN, OWN + 1024)], []))
+            break
+        e = r + 1
+        sact(R("SZ", 256 * e, 256 * e + 256), IND(*Zown, R("BL", 16, 32)))
+        sca("YW", oa, R("nzv", 0, 64))
+        sca("YW", ow, R("nzv", 64, 128))
+        vcopy(R("SY", 256 * e, 256 * e + 256), IND(*Yown, R("BL", 0, 16)))
+        need("G", "rdy%d" % e, 3)
+        send(e, "SZ", "ZW")
+        send(e, "SY", "YW")
+        vtt(R("d3", 0, 4), R("da", 0, 4), R("cl2", 15, 64, 16), O.mult)
+        sca("tNZM", oa, R("L2", 128, 192))
+        sca("tNZM", ow, R("L2", 0, 64))
+        vtt(R("VL", 0, 4), R("d3", 0, 4), R("alt", 0, 4), O.add)
+        vsum(C("cn"), a64("cm"))
+        vcopy(R("vl", 0, 4), R("VL", 0, 4))
+        vcopy(C("cnt"), C("cn"))
+        vcopy(R("L1", 0, 64), IND("tNB", 0, 1024, R("vl", 0, 4)))
+        pe([mm(R("pb7", 256, 257), a128("onesb"), C("cnt"), True, True)])
+        sca("tNBI", oqq, R("L2", 192, 256))
+        sca("tNBI", op, R("L2", 64, 128))
+        vcopy(R("L1", 64, 128), IND("tNZM", OWN, OWN + 1024, R("vl", 0, 4)))
+        vcopy(C("thi"), R("pb7", 256, 257))
+        step_lists()
+        vts(C("thj"), C("thi"), 31, None, O.bitwise_and)
+        sca(mt, oa, R("AQ", 64, 128))
+        vcopy(C("thc"), C("thj"))
+        sca(mt, ow, R("WP", 64, 128))
+        vts(a64("TH"), a64("nmB"), C("thc"), None, O.add)
+        sca("tIM", oqq, R("AQ", 0, 64))
+        sca("tIM", op, R("WP", 0, 64))
+        if r == 0:
+            vcopy(R("MF", OWN, OWN + 1024), R("tM", OWN, OWN + 1024))
+
+    total.update(cnt)
+    total["sl"] = nsl[0]
+    for s, v in total.items():
+        if max(seen[q].get(s, 0) for q in seen) < v:
+            g.wait_ge(T.sem[s], v)

@@ -1,16 +1,15 @@
-from concourse.bass import DstId, RemoteDMATransfer
 from concourse.mybir import AluOpType as O, AxisListType, ActivationFunctionType as AF
 
 F4, B2, I4, U2 = "float32", "bfloat16", "int32", "uint16"
 _W = {
-    B2: dict(ZW=1920, YW=1920, tX=1024, SY=512 + 256, SZ=768, Yt=1024, Zt=1024, ng=256, AD=1024, At=1024, Bt=1024, Bp=1024, T1=1024,
+    B2: dict(ZW=1920, YW=1920, tX=1024, SY=768, SZ=768, Yt=1024, Zt=1024, ng=512, AD=1024, At=1024, Bt=1024, Bp=1024, T1=1024,
              T2=1024, R1=1024, R2=1024, zz=128, xx=128, cl=128, nzv=128, EQ=640, gh=128, kz2=64, npr=64, WT=512, cnt=2,
              identb=128, identn=128, biasd=128, blkp=128, blkm=128, blkV=128, idV=128, idN=128, Es=144, W4=512, ones64=64,
              onesb=128),
-    F4: dict(MF=1152, mlf=256, nf=128, KT=64, Fs=64, OHt=64, OH=64, pr=128, mk=128, sc=128, WP=128, AQ=128, NR=128, mk2=128,
-             sc2=128, NLc=16, NLd=16, kz=64, TH=64, x1=64, sp=64, cm=64, cl2=64, VL=4, V5=4, oq=4, d1=4, d2=4, alt=4, da=4,
+    F4: dict(MF=1152, mlf=256, nf=128, KT=64, Fs=64, OHt=64, pr=128, mk=128, sc=128, WP=128, AQ=128, NR=128, mk2=128,
+             sc2=128, NLc=16, kz=64, TH=64, x1=64, sp=64, cm=64, cl2=64, VL=4, V5=4, oq=4, d1=4, d2=4, alt=4, da=4,
              d3=4, cn=2, thc=2, onesf=128, b1=128, blkf=128, ff=2, f15=2, itf=128, mask=128, reset=128, identf=128, q25=16,
-             s0=16, pwr=16, pm=16, pwc=2, c25=64, c00=64, thr=64, t1=64, mm1=64, thrM=64, nmB=64, c16f=4, lane4=4, lm16=16),
+             s0=16, pwr=16, pm=16, pwc=2, c25=64, c00=64, thr=64, t1=64, mm1=64, thrM=64, nmB=64, c16f=4, lane4=4),
     I4: dict(tNB=1024, tNZ=1024, tNZM=1152, tNBI=1152, tM=1152, tIM=1152, ml=256, bl=32, v5a=4, v5b=4, thi=2, thj=2, c_it=128,
              c_p=2, c_c16=4, fI=2),
     U2: dict(ML=128, BL=32, L1=128, LAQ=8, L2=256, LWP=8, OFF=16, vl=4),
@@ -19,10 +18,12 @@ SCRATCH = {n: ("sbuf", [128, w], d) for d in _W for n, w in _W[d].items()}
 for _i in range(8):
     SCRATCH["pb%d" % _i] = ("psum", [128, 512], F4)
 SEMAPHORES = ["cv", "cs", "cp", "cg", "ld_z", "ld_b", "ld_m", "ld_im", "ld_nz", "ld_nb", "ld_x", "ld_M", "ld_IM", "st_z", "st_m",
-              "aY0", "aY1", "aY2", "aZ0", "aZ1", "aZ2", "rdy1", "rdy2", "sl"]
+              "rdy1", "rdy2", "sl"] + ["%s%s%d" % (a, w, e) for a in "ab" for w in "YZ" for e in range(3)]
 N = 8
 OWN = 128
-CH = [(0, 16), (16, 40), (40, 64)]
+CFG = dict(CH=[(0, 24), (24, 44), (44, 64)],
+           YS=24,
+           AS=32)
 
 
 def rank_program(g, core, T, topo):
@@ -35,6 +36,7 @@ def rank_program(g, core, T, topo):
     total = {}
     seen = {q: {} for q in QUEUE}
     acc = {}
+    CH, YS, AS = CFG["CH"], CFG["YS"], CFG["AS"]
 
     def need(q, sem, val):
         if seen[q].get(sem, 0) < val:
@@ -125,7 +127,7 @@ def rank_program(g, core, T, topo):
     def pe(ms):
         emit("P", [m[0] for m in ms], [m[1] for m in ms], [x for m in ms for x in (m[2], m[3])])
 
-    def load(q, sem, n, o, in_ap, tot):
+    def load(q, sem, o, in_ap, tot):
         order(q, [], o[1])
         QUEUE[q].dma_start(out=o[0], in_=in_ap).then_inc(T.sem[sem], 16)
         total[sem] = 16 * tot
@@ -136,27 +138,22 @@ def rank_program(g, core, T, topo):
         QUEUE[q].dma_start(out=out_ap, in_=i[0]).then_inc(T.sem[sem], 16)
         total[sem] = 16
 
-    load("S", "ld_z", 0, R("ZW", OWN, OWN + 1024), T.z[:], 1)
-    load("S", "ld_b", 0, R("bl", 0, 16), T.bx[:], 2)
-    load("S", "ld_b", 0, R("bl", 16, 32), T.bz[:], 2)
-    load("S", "ld_nz", 0, R("tNZ", 0, 1024), T.nz[:], 1)
-    load("S", "ld_nb", 0, R("tNB", 0, 1024), T.nb[:], 1)
-    for k in range(8):
-        load("Y", "ld_m", 0, (T.ml[0:64, 16 * k:16 * k + 16], [("ml", 16 * k, 16 * k + 16)], []), T.m[k:k + 1, :], 8)
-    for k in range(8):
-        load("Y", "ld_im", 0, (T.ml[0:64, 128 + 16 * k:144 + 16 * k], [("ml", 128 + 16 * k, 144 + 16 * k)], []), T.im[k:k + 1, :], 8)
-    for f in range(16):
-        load("Y", "ld_IM", 0, (T.tIM[f:128:16, OWN:OWN + 1024], [("tIM", OWN, OWN + 1024)], []), T.im[:], 16) if False else None
-    load("Y", "ld_x", 0, R("tX", 0, 1024), T.x[:], 1)
+    def lists(a, sem, src):
+        for k in range(8):
+            c = a + 16 * k
+            load("Y", sem, (T.ml[0:64, c:c + 16], [("ml", c, c + 16)], []), src[k:k + 1, :], 8)
 
     def spread(sem, n, src):
-        order("Y", [], [(n, OWN, OWN + 1024)])
         for f in range(16):
-            g.sync.dma_start(out=T[n][f:128:16, OWN:OWN + 1024], in_=src[:]).then_inc(T.sem[sem], 16)
-        total[sem] = 256
+            load("Y", sem, (T[n][f:128:16, OWN:OWN + 1024], [(n + "_" + str(f), 0, 1)], []), src[:], 16)
         record("D" + sem, [], [(n, OWN, OWN + 1024)], sem, 256)
-    spread("ld_IM", "tIM", T.im)
-    spread("ld_M", "tM", T.m)
+    load("S", "ld_b", R("bl", 0, 16), T.bx[:], 2)
+    load("S", "ld_b", R("bl", 16, 32), T.bz[:], 2)
+    lists(0, "ld_m", T.m)
+    load("S", "ld_z", R("ZW", OWN, OWN + 1024), T.z[:], 1)
+    load("Y", "ld_nz", R("tNZ", 0, 1024), T.nz[:], 1)
+    lists(128, "ld_im", T.im)
+    load("Y", "ld_nb", R("tNB", 0, 1024), T.nb[:], 1)
 
     def giota(o, pat, ch):
         emit("G", [lambda: g.iota(o[0], pat, 0, ch)], [o], [])
@@ -165,48 +162,126 @@ def rank_program(g, core, T, topo):
         emit("G", [lambda: g.affine_select(o[0], i[0], pat, O.is_ge, 0.0, base, ch)], [o], [i])
     a128 = lambda n: R(n, 0, 128)
     a64 = lambda n: R(n, 0, 64)
+    MP = R("pb6", 256, 384)
     vset(a128("onesf"), 1.0)
     giota(R("c_p", 0, 2), [[0, 2]], 1)
     giota(a128("c_it"), [[0, 8], [1, 16]], 0)
     gsel(a128("b1"), a128("onesf"), [[-16, 8], [0, 16]], 0, 1)
     gsel(a128("blkf"), a128("b1"), [[16, 8], [0, 16]], 15, -1)
     giota(R("c_c16", 0, 4), [[16, 4]], 0)
+    vset(a64("ones64"), 1.0)
+    vset(R("Es", 0, 144), 0.0)
+    vset(a64("c25"), 0.25)
+    vset(a64("c00"), 0.0)
     vts(R("fI", 0, 2), R("c_p", 0, 2), 15, None, O.bitwise_and)
-    vcopy(R("ff", 0, 2), R("fI", 0, 2))
     vcopy(a128("itf"), a128("c_it"))
-    vts(a128("mask"), a128("itf"), C("ff"), None, O.is_equal)
+    vcopy(R("ff", 0, 2), R("fI", 0, 2))
     vts(a128("reset"), a128("itf"), 0.0, None, O.is_gt)
+    vts(a128("mask"), a128("itf"), C("ff"), None, O.is_equal)
+    vts(C("f15"), C("ff"), -1.0, 15.0, O.mult, O.add)
+    vscan(a64("thr"), a64("c25"), a64("c00"), 3.0 * 4.0 ** 33, O.mult, O.add)
     vtt(a128("identf"), a128("blkf"), a128("mask"), O.mult)
+    vcopy(MP, a128("mask"))
+    vts(R("Es", 15, 143, 16), R("blkf", 0, 128, 16), 16.0, None, O.mult)
+    vts(a128("identn"), a128("identf"), -1.0, None, O.mult)
+    vcopy(a128("identb"), a128("identf"))
+    vcopy(R("BL", 0, 32), R("bl", 0, 32))
+    vts(a128("biasd"), a128("identf"), C("f15"), None, O.mult)
+    vts(R("q25", 0, 16), R("reset", 0, 16), 0.25, None, O.mult)
+    vts(R("s0", 0, 16), R("reset", 0, 16), -1.0, 1.0, O.mult, O.add)
+    vts(a64("mm1"), a64("mask"), -1.0, None, O.add)
+    vscan(R("pwr", 0, 16), R("q25", 0, 16), R("s0", 0, 16), 0.0, O.mult, O.add)
+    vtt(a64("t1"), a64("thr"), a64("mask"), O.mult)
+    vtt(R("pm", 0, 16), R("pwr", 0, 16), R("mask", 0, 16), O.mult)
+    vts(a64("nmB"), a64("mask"), -float(2 ** 24), float(2 ** 24), O.mult, O.add)
+    vsum(C("pwc"), R("pm", 0, 16))
+    vtt(a64("thrM"), a64("t1"), a64("mm1"), O.add)
+    vcopy(R("c16f", 0, 4), R("c_c16", 0, 4))
+    vts(R("lane4", 0, 4), R("c16f", 0, 4), C("ff"), None, O.add)
+    for c in range(4):
+        vts(R("W4", 128 * c, 128 * c + 128), a128("blkf"), C("pwc"), 4.0 ** (32 - 16 * c), O.mult, O.mult)
+    vts(R("VL", 0, 4), R("lane4", 0, 4), 16.0, None, O.mult)
+    sact(a128("blkp"), a128("blkf"), AF.Copy, 2.0)
+    sact(a128("blkm"), a128("blkf"), AF.Copy, -2.0)
+    sact(a128("blkV"), a128("blkf"), AF.Copy, -float(2 ** 20))
+    sact(a128("idV"), a128("identf"), AF.Copy, -float(2 ** 20))
+    sact(a128("idN"), a128("identf"), AF.Copy, float(2 ** 70))
+    sact(a128("onesb"), a128("onesf"))
 
-    peers_to = [T.cores[(rank - d) % N] for d in (1, 2, 3)]
-    peers_from = [T.cores[(rank + d) % N] for d in (1, 2, 3)]
-    emask = 0xFFFF
-    for d in peers_to:
-        emask &= topo.mask(core, d)
-    neng = bin(emask).count("1")
+    def near(c):
+        return topo.cores_of(c)
+
+    def wmask(c, d):
+        m = topo.mask(c, d)
+        if d in near(c):
+            for o in T.cores:
+                if o not in near(c):
+                    m &= ~topo.mask(c, o)
+        return m
+
+    def ones(m):
+        return bin(m).count("1")
+
+    def plan(s):
+        ds = [(d, T.cores[(T.rank_of(s) - d) % N]) for d in (1, 2, 3)]
+        rel = []
+        for (d, t) in ds:
+            twin = [(e, u) for (e, u) in ds if u != t and u in near(t)]
+            if t not in near(s) and twin and topo.die(t) != topo.die(s):
+                rel.append((twin[0][1], twin[0][0], t, d))
+        far = [x[2] for x in rel]
+        lead = [x[0] for x in rel]
+        direct = [(d, t, t in lead) for (d, t) in ds if t not in far]
+        return sorted(direct, key=lambda x: not x[2]), rel
+    plans = {s: plan(s) for s in T.cores}
+    duty = [(e, t, d) for s in T.cores for (u, e, t, d) in plans[s][1] if u == core]
+
+    def targets(s):
+        return [t for (d, t, l) in plans[s][0]] + [t for p in plans.values() for (u, e, t, d) in p[1] if u == s]
+    writers = [s for s in T.cores if core in targets(s)]
+    tell = len(set(targets(core)))
+    come = []
+    for s in T.cores:
+        for (d, t, l) in plans[s][0]:
+            if t == core:
+                come.append(("b" if l else "a", d, ones(wmask(s, core))))
+        for (u, e, t, d) in plans[s][1]:
+            if t == core:
+                come.append(("a", d, ones(wmask(u, core))))
     nsl = [0]
-    allsem = {}
+    block = lambda d: (OWN + 1024 + 256 * (d - 1), OWN + 1280 + 256 * (d - 1))
 
-    def send(e, n, win):
-        i = R(n, 256 * e, 256 * e + 256)
-        order("G", i[1], [])
-        ids, dsts = [], []
-        for d in (1, 2, 3):
-            rid, pid = topo.addr(peers_to[d - 1], core)
-            ids.append(DstId(rid=rid, pnc=pid))
-            c = OWN + 1024 + 256 * (d - 1)
-            dsts.append(T[win][:, c:c + 256])
-        s = "a%s%d" % (win[0], e)
-        g.remote_dma_fused([RemoteDMATransfer(dst_ids=ids, dma_engine_mask=emask, remote_sem=T.sem[s], srcs=[i[0]], dsts=dsts)],
-                           local_sem=T.sem.sl)
-        nsl[0] += neng
-        total[s] = 3 * neng
-        record("A", [], [(win, OWN + 1024, OWN + 1792)], s, 3 * neng)
+    def put(dst, win, d, src, sem):
+        order("G", src[1], [])
+        rid, pid = topo.addr(dst, core)
+        a, b = block(d)
+        m = wmask(core, dst)
+        g.remote_dma(out_ap=T[win][:, a:b], in_ap=src[0], remote_sem=T.sem[sem], local_sem=T.sem.sl, pid=pid, routing_id=rid,
+                     dma_engine_mask=m)
+        nsl[0] += ones(m)
 
     Zown, Zall = ("ZW", OWN, OWN + 1024), ("ZW", OWN, OWN + 1792)
     Yown, Yall = ("YW", OWN, OWN + 1024), ("YW", OWN, OWN + 1792)
 
-    vcopy(R("BL", 0, 32), R("bl", 0, 32))
+    def borders(e):
+        vcopy(R("SY", 256 * e, 256 * e + 128), IND(*Yown, R("BL", 0, 8)))
+        sact(R("SY", 256 * e + 128, 256 * e + 256), IND(*Yown, R("BL", 8, 16)))
+        two = (("SZ", "ZW", "Z%d" % e), ("SY", "YW", "Y%d" % e))
+        todo = [(w, x) for x in plans[core][0] for w in two]
+        if e == 0:
+            todo = [(w, x) for w in two for x in plans[core][0]]
+        for (n, win, s), (d, t, l) in todo:
+            put(t, win, d, R(n, 256 * e, 256 * e + 256), ("b" if l else "a") + s)
+        for (n, win, s) in two:
+            for k in "ab":
+                v = sum(x[2] for x in come if x[0] == k)
+                total[k + s] = v
+                for x in come:
+                    if x[0] == k:
+                        record("A", [], [(win,) + block(x[1])], k + s, v)
+            for (b, t, d) in duty:
+                put(t, win, d, R(win, *block(b)), "a" + s)
+
     sact(R("SZ", 0, 256), IND(*Zown, R("BL", 16, 32)))
     mlp = lambda n, a: (T[n][0:64, a:a + 128], [(n, a, a + 128)], [])
     id64 = (T.identf[0:64, 0:64], [("identf", 0, 128)], [])
@@ -219,46 +294,16 @@ def rank_program(g, core, T, topo):
     mlist(0, "pb0")
     vcopy(R("YW", OWN, OWN + 512), IND(*Zown, R("ML", 0, 32)))
     sact(R("YW", OWN + 512, OWN + 1024), IND(*Zown, R("ML", 32, 64)))
-    vcopy(R("SY", 0, 256), IND(*Yown, R("BL", 0, 16)))
-    send(0, "SZ", "ZW")
-    send(0, "SY", "YW")
-    vts(a128("identn"), a128("identf"), -1.0, None, O.mult)
-    vcopy(a128("identb"), a128("identf"))
+    borders(0)
+    need("Y", "aZ0", total["aZ0"])
+    spread("ld_IM", "tIM", T.im)
+    spread("ld_M", "tM", T.m)
+    load("Y", "ld_x", R("tX", 0, 1024), T.x[:], 1)
     vcopy(R("tNZM", OWN, OWN + 1024), IND("tNZ", 0, 1024, R("ML", 0, 64)))
     mlist(128, "pb1")
     vcopy(R("L1", 64, 128), R("tNZM", OWN, OWN + 1024, 16))
     vcopy(R("L1", 0, 64), R("tNB", 0, 1024, 16))
-    vts(C("f15"), C("ff"), -1.0, 15.0, O.mult, O.add)
-    vts(a128("biasd"), a128("identf"), C("f15"), None, O.mult)
-    vset(a64("ones64"), 1.0)
-    vset(R("Es", 0, 144), 0.0)
-    vts(R("Es", 15, 143, 16), R("blkf", 0, 128, 16), 16.0, None, O.mult)
     vcopy(R("tNBI", OWN, OWN + 1024), IND("tNB", 0, 1024, R("ML", 64, 128)))
-    sact(a128("blkp"), a128("blkf"), AF.Copy, 2.0)
-    sact(a128("blkm"), a128("blkf"), AF.Copy, -2.0)
-    sact(a128("blkV"), a128("blkf"), AF.Copy, -float(2 ** 20))
-    sact(a128("idV"), a128("identf"), AF.Copy, -float(2 ** 20))
-    sact(a128("idN"), a128("identf"), AF.Copy, float(2 ** 70))
-    sact(a128("onesb"), a128("onesf"))
-    vts(R("q25", 0, 16), R("reset", 0, 16), 0.25, None, O.mult)
-    vts(R("s0", 0, 16), R("reset", 0, 16), -1.0, 1.0, O.mult, O.add)
-    vset(a64("c25"), 0.25)
-    vset(a64("c00"), 0.0)
-    vscan(R("pwr", 0, 16), R("q25", 0, 16), R("s0", 0, 16), 0.0, O.mult, O.add)
-    vscan(a64("thr"), a64("c25"), a64("c00"), 3.0 * 4.0 ** 33, O.mult, O.add)
-    vtt(R("pm", 0, 16), R("pwr", 0, 16), R("mask", 0, 16), O.mult)
-    vts(a64("mm1"), a64("mask"), -1.0, None, O.add)
-    vsum(C("pwc"), R("pm", 0, 16))
-    vtt(a64("t1"), a64("thr"), a64("mask"), O.mult)
-    vts(a64("nmB"), a64("mask"), -float(2 ** 24), float(2 ** 24), O.mult, O.add)
-    for c in range(4):
-        vts(R("W4", 128 * c, 128 * c + 128), a128("blkf"), C("pwc"), 4.0 ** (32 - 16 * c), O.mult, O.mult)
-    vtt(a64("thrM"), a64("t1"), a64("mm1"), O.add)
-    vcopy(R("c16f", 0, 4), R("c_c16", 0, 4))
-    vts(R("lane4", 0, 4), R("c16f", 0, 4), C("ff"), None, O.add)
-    for n in range(4):
-        vts(R("lm16", 4 * n, 4 * n + 4), R("lane4", 0, 4), -float(OWN), None, O.add)
-    vts(R("VL", 0, 4), R("lane4", 0, 4), 16.0, None, O.mult)
 
     def step_lists():
         vcopy(a128("nf"), a128("L1"))
@@ -270,77 +315,99 @@ def rank_program(g, core, T, topo):
     for r in range(3):
         mt = "tM" if r == 0 else "MF"
         more = r < 2
-        for j, (a, b) in enumerate(CH):
-            vcopy(R("Yt", 16 * a, 16 * b), IND(*Yall, R("L1", a, b)))
+        for (a, b) in CH:
             sact(R("Zt", 16 * a, 16 * b), IND(*Zall, R("L1", 64 + a, 64 + b)))
+            b = min(b, 64 - YS)
+            if a < b:
+                vcopy(R("Yt", 16 * a, 16 * b), IND(*Yall, R("L1", a, b)))
+        sact(R("Yt", 1024 - 16 * YS, 1024), IND(*Yall, R("L1", 64 - YS, 64)))
+        for j, (a, b) in enumerate(CH):
             o = R("pb%d" % j, 0, 16 * (b - a))
             pe([mm(o, a128("identb"), R("Yt", 16 * a, 16 * b), True, False),
                 mm(o, a128("identn"), R("Zt", 16 * a, 16 * b), False, True)])
-        vts(R("ng", 0, 256), R("pb0", 0, 256), -1.0, None, O.mult)
-        vtt(R("AD", 0, 256), R("pb0", 0, 256), R("ng", 0, 256), O.max)
+        c0 = 16 * CH[0][1]
+        vts(R("ng", 0, c0), R("pb0", 0, c0), -1.0, None, O.mult)
+        vtt(R("AD", 0, c0), R("pb0", 0, c0), R("ng", 0, c0), O.max)
         for j in (1, 2):
             a, b = CH[j]
             sact(R("AD", 16 * a, 16 * b), R("pb%d" % j, 0, 16 * (b - a)), AF.Abs)
         K = R("pb3", 0, 64)
         pe([mm(K, a128("biasd"), a64("ones64"), True, False)] +
            [mm(K, R("Es", 15 - k, 143 - k), R("AD", k, 1024, 16), False, k == 15) for k in range(16)])
+        OH = R("pb5", 0, 64)
         vtr(a64("KT"), K)
         vscan(a64("Fs"), a64("reset"), a64("KT"), 0.0, O.mult, O.max)
         for s in range(4):
             vts(R("OHt", 16 * s, 16 * s + 16), R("KT", 16 * s, 16 * s + 16), C("Fs", 16 * s + 15), None, O.is_equal)
-        vtr(a64("OH"), a64("OHt"))
-        vtt(R("pr", 0, 64), a64("OH"), R("nf", 0, 64), O.mult)
-        vtt(R("pr", 64, 128), a64("OH"), R("nf", 64, 128), O.mult)
+        vtr(OH, a64("OHt"))
+        vtt(R("pr", 0, 64), OH, R("nf", 0, 64), O.mult)
+        vtt(R("pr", 64, 128), OH, R("nf", 64, 128), O.mult)
         ROW = R("pb4", 0, 128)
         pe([mm(ROW, a128("blkf"), a128("pr"), True, True)])
+        vts(a64("kz"), K, 16.0, None, O.is_lt)
+        vtt(a64("kz2"), a64("kz"), OH, O.mult)
         vtt(a128("mk"), ROW, a128("mask"), O.mult)
         vscan(a128("sc"), a128("reset"), a128("mk"), 0.0, O.mult, O.add)
         vts(R("LAQ", 0, 8), R("sc", 15, 128, 16), 1023.0, None, O.min)
         la, lq = R("LAQ", 0, 4), R("LAQ", 4, 8)
         vcopy(R("L2", 0, 64), IND("tNZM", OWN, OWN + 1024, la))
-        for h in (0, 1):
-            sact(R("Bt", 512 * h, 512 * h + 512), IND(*Zall, R("L2", 32 * h, 32 * h + 32)))
         vcopy(R("L2", 64, 128), IND("tNBI", OWN, OWN + 1024, lq))
-        sact(R("At", 512, 1024), IND(*Yall, R("L2", 96, 128)))
         vcopy(R("L2", 128, 192), IND("tNZ", 0, 1024, lq))
-        for h in (0, 1):
-            sact(R("Bp", 512 * h, 512 * h + 512), IND(*Zall, R("L2", 128 + 32 * h, 160 + 32 * h)))
-        vcopy(R("At", 0, 512), IND(*Yall, R("L2", 64, 96)))
+        for n, c in (("Bt", 0), ("Bp", 128)):
+            for h in (0, 1):
+                sact(R(n, 512 * h, 512 * h + 512), IND(*Zall, R("L2", c + 32 * h, c + 32 * h + 32)))
+        sact(R("At", 1024 - 16 * AS, 1024), IND(*Yall, R("L2", 128 - AS, 128)))
+        vcopy(R("At", 0, 1024 - 16 * AS), IND(*Yall, R("L2", 64, 128 - AS)))
         vcopy(R("L2", 192, 256), IND("tNB", 0, 1024, la))
         vcopy(R("WP", 0, 64), IND("tIM", OWN, OWN + 1024, lq))
         vcopy(R("WP", 64, 128), IND(mt, OWN, OWN + 1024, la))
         vts(a128("gh"), ROW, 1024.0, None, O.is_ge)
-        vts(a64("kz"), K, 16.0, None, O.is_lt)
-        vtt(a64("kz2"), a64("kz"), a64("OH"), O.mult)
-        dif = []
-        for j, (bk, src, h) in enumerate([("pb0", "Bt", 0), ("pb1", "Bt", 1), ("pb2", "Bp", 0), ("pb5", "Bp", 1)]):
-            s = slice(512 * h, 512 * h + 512)
-            o = R(bk, 0, 512)
-            pe([mm(o, a128("identb"), R(src, s.start, s.stop), True, False),
-                mm(o, a128("identn"), R("At", s.start, s.stop), False, True)])
-            dif.append(o)
+        vtt(a128("mk2"), a128("WP"), MP, O.mult)
         sact(a128("AQ"), ROW)
         sact(R("NR", 0, 128, 2), R("AQ", 0, 64))
         sact(R("NR", 1, 128, 2), R("WP", 0, 64))
-        for h in (0, 1):
-            sact(R("R1", 512 * h, 512 * h + 512), dif[h], AF.Relu)
-        for h in (0, 1):
-            sact(R("R2", 512 * h, 512 * h + 512), dif[2 + h], AF.Relu)
-        vtt(a128("mk2"), a128("WP"), a128("mask"), O.mult)
         vtt(R("T1", 0, 1024), IND(*Yall, R("L2", 192, 256)), R("Bt", 0, 1024), O.max)
         vscan(a128("sc2"), a128("reset"), a128("mk2"), 0.0, O.mult, O.add)
-        vts(R("NLc", 0, 8), R("sc", 15, 128, 16), 1023.0, None, O.min)
-        vcopy(R("NLc", 8, 16), R("sc2", 15, 128, 16))
+        vts(R("NLc", 0, 8), R("sc", 15, 128, 16), 1023.0, float(OWN), O.min, O.add)
+        vts(R("NLc", 8, 16), R("sc2", 15, 128, 16), float(OWN), None, O.add)
         vcopy(R("LWP", 0, 8), R("sc2", 15, 128, 16))
         vtt(R("T2", 0, 1024), IND(*Yall, R("L2", 192, 256)), R("Bp", 0, 1024), O.max)
         if more:
             need("G", "cv", cnt["cv"])
             need("G", "cs", max(e[5] for w in ("ZW", "YW") for e in acc[w] if e[3] == "S"))
-            for d in peers_from:
+            need("G", "sl", nsl[0])
+            for d in writers:
                 rid, pid = topo.addr(d, core)
                 g.remote_sem_update(T.sem["rdy%d" % (r + 1)], T.sem.sl, pid, rid, 1 << topo.engines(core, d)[0])
                 nsl[0] += 1
-            total["rdy%d" % (r + 1)] = 3
+            total["rdy%d" % (r + 1)] = tell
+        Gn = R("pb6", 0, 64)
+        dif = {}
+
+        def diff(bk, src, h):
+            a, b = 512 * h, 512 * h + 512
+            o = R(bk, 0, 512)
+            pe([mm(o, a128("identb"), R(src, a, b), True, False), mm(o, a128("identn"), R("At", a, b), False, True)])
+            dif[src, h] = o
+
+        def term(n, l):
+            pe([mm(Gn, a128(l), R(n, k, 1024, 16), False, n == "R2" and k == 15) for k in range(16)])
+        diff("pb0", "Bt", 0)
+        diff("pb2", "Bp", 0)
+        pe([mm(Gn, a128("idV"), R("gh", 0, 64), True, False), mm(Gn, a128("idV"), R("gh", 64, 128), False, False),
+            mm(Gn, a128("blkV"), a64("kz2"), False, False)])
+        term("T1", "blkp")
+        diff("pb1", "Bt", 1)
+        diff("pb5", "Bp", 1)
+        for (n, src, h) in (("R1", "Bt", 0), ("R2", "Bp", 0), ("R1", "Bt", 1), ("R2", "Bp", 1)):
+            o = R(n, 512 * h, 512 * h + 512)
+            if n == "R1" and h == 0:
+                vts(o, dif[src, h], 0.0, None, O.max)
+            else:
+                sact(o, dif[src, h], AF.Relu)
+        term("T2", "blkm")
+        term("R1", "blkm")
+        term("R2", "blkp")
         sact(R("zz", 0, 64), IND(*Zown, lq))
         sact(R("xx", 0, 64), IND("tX", 0, 1024, la))
         sact(R("zz", 64, 128), IND(*Zown, R("LWP", 4, 8)))
@@ -352,46 +419,32 @@ def rank_program(g, core, T, topo):
                 vts(R("EQ", at, at + w), R("NR", 32 * c, 128), col, None, O.is_equal)
                 eqs.append((c, at, w))
                 at += w
-        vtt(R("NLd", 0, 16), R("NLc", 0, 16), R("lm16", 0, 16), O.subtract)
+        vtt(a64("x1"), Gn, a64("TH") if r else a64("nmB"), O.is_gt)
+        vscan(a64("sp"), a64("reset"), a64("x1"), 0.0, O.mult, O.add)
+        for c in range(4):
+            vts(R("WT", 128 * c, 128 * c + 128), R("W4", 128 * c, 128 * c + 128), C("sp", 16 * c + 15), None, O.mult)
+        vts(a64("npr"), Gn, C("thc") if r else 0.0, None, O.is_le)
+        xz = R("pb4", 128, 256)
+        pe([mm(xz, a128("identb"), a128("xx"), True, False), mm(xz, a128("identn"), a128("zz"), False, True)])
+        vts(a128("cl"), xz, -1.0, 1.0, O.max, O.min)
+        CS = R("pb7", 0, 64)
+        for c in range(4):
+            pe([mm(R("pb7", 16 * c, 64), R("WT", 128 * c, 128 * c + 128), R("EQ", at + nm, at + w, 2),
+                   c == 0 and (at, nm) == (0, 0), False) for (c2, at, w) in eqs if c2 == c for nm in (0, 1)])
+        pe([mm(CS, a128("idN"), a64("npr"), False, True)])
+        nzp = R("pb3", 128, 256)
+        pe([mm(nzp, a128("identb"), a128("zz"), True, False), mm(nzp, a128("identb"), a128("cl"), False, True)])
+        sact(a128("nzv"), nzp)
         if more:
             vts(R("oq", 0, 4), R("sc", 79, 128, 16), 1024.0, None, O.is_lt)
             vtt(R("d1", 0, 4), R("sc2", 15, 64, 16), R("V5", 0, 4), O.subtract)
             vtt(R("d2", 0, 4), R("d1", 0, 4), R("oq", 0, 4), O.mult)
             vtt(R("alt", 0, 4), R("d2", 0, 4), R("V5", 0, 4), O.add)
             vtt(R("da", 0, 4), R("sc", 15, 64, 16), R("alt", 0, 4), O.subtract)
-        Gn = R("pb6", 0, 64)
-        pe([mm(Gn, a128("idV"), R("gh", 0, 64), True, False), mm(Gn, a128("idV"), R("gh", 64, 128), False, False),
-            mm(Gn, a128("blkV"), a64("kz2"), False, False)])
-        for n, l in (("T1", "blkp"), ("R1", "blkm"), ("T2", "blkm"), ("R2", "blkp")):
-            pe([mm(Gn, a128(l), R(n, k, 1024, 16), False, n == "R2" and k == 15) for k in range(16)])
-        if r:
-            vtt(a64("x1"), Gn, a64("TH"), O.is_gt)
-            vts(a64("npr"), Gn, C("thc"), None, O.is_le)
-        else:
-            vtt(a64("x1"), Gn, a64("nmB"), O.is_gt)
-            vts(a64("npr"), Gn, 0.0, None, O.is_le)
-        vscan(a64("sp"), a64("reset"), a64("x1"), 0.0, O.mult, O.add)
-        for c in (0, 1):
-            vts(R("WT", 128 * c, 128 * c + 128), R("W4", 128 * c, 128 * c + 128), C("sp", 16 * c + 15), None, O.mult)
-        for c in (2, 3):
-            sact(R("WT", 128 * c, 128 * c + 128), R("W4", 128 * c, 128 * c + 128), AF.Copy, C("sp", 16 * c + 15))
-        xz = R("pb4", 128, 256)
-        pe([mm(xz, a128("identb"), a128("xx"), True, False), mm(xz, a128("identn"), a128("zz"), False, True)])
-        vts(a128("cl"), xz, -1.0, 1.0, O.max, O.min)
-        CS = R("pb7", 0, 64)
-        ms = [mm(CS, a128("idN"), a64("npr"), True, False)]
-        for (c, at, w) in eqs[::-1]:
-            for nm in (0, 1):
-                ms.append([R("pb7", 16 * c, 64), R("WT", 128 * c, 128 * c + 128), R("EQ", at + nm, at + w, 2)])
-        ms = ms[:1] + [mm(o, l, x, False, i == len(ms) - 2) for i, (o, l, x) in enumerate(ms[1:])]
-        pe(ms)
-        nzp = R("pb3", 128, 256)
-        pe([mm(nzp, a128("identb"), a128("zz"), True, False), mm(nzp, a128("identb"), a128("cl"), False, True)])
-        sact(a128("nzv"), nzp)
         vtt(a64("cm"), CS, a64("thrM"), O.is_le)
         vscan(a64("cl2"), a64("reset"), a64("cm"), 0.0, O.mult, O.add)
         for c in range(4):
-            vts(R("OFF", c, 16, 4), R("NLd", c, 16, 4), C("cl2", 16 * c + 15), C("lane4", c), O.mult, O.add)
+            vts(R("OFF", c, 16, 4), R("NLc", c, 16, 4), C("cl2", 16 * c + 15), C("lane4", c), O.mult, O.max)
         oa, oqq, ow, op = [R("OFF", 4 * n, 4 * n + 4) for n in range(4)]
         sca = lambda n, off, d: vcopy(IND(n, 0, OWN + 1024, off), d)
         sca("ZW", oqq, R("nzv", 0, 64))
@@ -406,10 +459,8 @@ def rank_program(g, core, T, topo):
         sact(R("SZ", 256 * e, 256 * e + 256), IND(*Zown, R("BL", 16, 32)))
         sca("YW", oa, R("nzv", 0, 64))
         sca("YW", ow, R("nzv", 64, 128))
-        vcopy(R("SY", 256 * e, 256 * e + 256), IND(*Yown, R("BL", 0, 16)))
-        need("G", "rdy%d" % e, 3)
-        send(e, "SZ", "ZW")
-        send(e, "SY", "YW")
+        need("G", "rdy%d" % e, tell)
+        borders(e)
         vtt(R("d3", 0, 4), R("da", 0, 4), R("cl2", 15, 64, 16), O.mult)
         sca("tNZM", oa, R("L2", 128, 192))
         sca("tNZM", ow, R("L2", 0, 64))
@@ -419,9 +470,9 @@ def rank_program(g, core, T, topo):
         vcopy(C("cnt"), C("cn"))
         vcopy(R("L1", 0, 64), IND("tNB", 0, 1024, R("vl", 0, 4)))
         pe([mm(R("pb7", 256, 257), a128("onesb"), C("cnt"), True, True)])
+        vcopy(R("L1", 64, 128), IND("tNZM", OWN, OWN + 1024, R("vl", 0, 4)))
         sca("tNBI", oqq, R("L2", 192, 256))
         sca("tNBI", op, R("L2", 64, 128))
-        vcopy(R("L1", 64, 128), IND("tNZM", OWN, OWN + 1024, R("vl", 0, 4)))
         vcopy(C("thi"), R("pb7", 256, 257))
         step_lists()
         vts(C("thj"), C("thi"), 31, None, O.bitwise_and)

from concourse.mybir import AluOpType as O, AxisListType, ActivationFunctionType as AF

F4, B2, I4, U2 = "float32", "bfloat16", "int32", "uint16"
_W = {
    B2: dict(ZW=1920, YW=1920, tX=1024, SY=768, SZ=768, Yt=1024, Zt=1024, ng=512, AD=1024, At=1024, Bt=1024, Bp=1024, T1=1024,
             T2=1024, R1=1024, R2=1024, zz=128, xx=128, cl=128, nzv=128, EQ=640, gh=128, kz2=64, npr=64, WT=512, cnt=2,
             identb=128, identn=128, biasd=128, blkp=128, blkm=128, blkV=128, idV=128, idN=128, Es=144, W4=512, ones64=64,
             onesb=128),
    F4: dict(MF=1152, mlf=256, nf=128, KT=64, Fs=64, OHt=64, pr=128, mk=128, sc=128, WP=128, AQ=128, NR=128, mk2=128,
             sc2=128, NLc=16, kz=64, TH=64, x1=64, sp=64, cm=64, cl2=64, VL=4, V5=4, oq=4, d1=4, d2=4, alt=4, da=4,
             d3=4, cn=2, thc=2, onesf=128, b1=128, blkf=128, ff=2, f15=2, itf=128, mask=128, reset=128, identf=128, q25=16,
             s0=16, pwr=16, pm=16, pwc=2, c25=64, c00=64, thr=64, t1=64, mm1=64, thrM=64, nmB=64, c16f=4, lane4=4),
    I4: dict(tNB=1024, tNZ=1024, tNZM=1152, tNBI=1152, tM=1152, tIM=1152, ml=256, bl=32, v5a=4, v5b=4, thi=2, thj=2, c_it=128,
             c_p=2, c_c16=4, fI=2),
    U2: dict(ML=128, BL=32, L1=128, LAQ=8, L2=256, LWP=8, OFF=16, vl=4),
}
SCRATCH = {n: ("sbuf", [128, w], d) for d in _W for n, w in _W[d].items()}
for _i in range(8):
    SCRATCH["pb%d" % _i] = ("psum", [128, 512], F4)
SEMAPHORES = ["cv", "cs", "cp", "cg", "ld_z", "ld_b", "ld_m", "ld_im", "ld_nz", "ld_nb", "ld_x", "ld_M", "ld_IM", "st_z", "st_m",
              "rdy1", "rdy2", "sl"] + ["%s%s%d" % (a, w, e) for a in "ab" for w in "YZ" for e in range(3)]
N = 8
OWN = 128
CFG = dict(CH=[(0, 24), (24, 44), (44, 64)],
           YS=24,
           AS=32)


def rank_program(g, core, T, topo):
    rank = T.rank_of(core)
    if rank is None:
        return
    QUEUE = {"V": g.vector, "S": g.scalar, "P": g.tensor, "G": g, "Y": g.sync}
    SEM = {"V": "cv", "S": "cs", "P": "cp", "G": "cg"}
    cnt = {"cv": 0, "cs": 0, "cp": 0, "cg": 0}
    total = {}
    seen = {q: {} for q in QUEUE}
    acc = {}
    CH, YS, AS = CFG["CH"], CFG["YS"], CFG["AS"]

    def need(q, sem, val):
        if seen[q].get(sem, 0) < val:
            QUEUE[q].wait_ge(T.sem[sem], val)
            seen[q][sem] = val

    def order(q, reads, writes):
        w = {}
        for kind, regs in (("r", reads), ("w", writes)):
            for (n, a, b) in regs:
                ps = n[:2] == "pb"
                for (a2, b2, k2, q2, s2, v2) in acc.get(n, ()):
                    if ps:
                        if q2 == q and (q == "P" or (kind == "r" and k2 == "r")):
                            continue
                    else:
                        if (kind == "r" and k2 == "r") or b2 <= a or b <= a2:
                            continue
                    w[s2] = max(w.get(s2, 0), v2)
        for s, v in w.items():
            need(q, s, v)

    def record(q, reads, writes, sem, val):
        for kind, regs in (("r", reads), ("w", writes)):
            for (n, a, b) in regs:
                l = [e for e in acc.get(n, []) if not (e[0] == a and e[1] == b and e[2] == kind and e[3] == q)]
                l.append((a, b, kind, q, sem, val))
                acc[n] = l

    def emit(q, calls, outs, ins):
        reads = [r for i in ins for r in i[1] + i[2]] + [r for o in outs for r in o[2]]
        writes = [r for o in outs for r in o[1]]
        order(q, reads, writes)
        for c in calls:
            last = c()
        s = SEM[q]
        cnt[s] += 1
        last.then_inc(T.sem[s], 1)
        record(q, reads, writes, s, cnt[s])

    def R(n, a, b, s=1):
        return (T[n][:, a:b] if s == 1 else T[n][:, a:b:s], [(n, a, b)], [])

    def C(n, c=0):
        return R(n, c, c + 1)

    def IND(n, a, b, off):
        return (T[n][:, a:b].indirect(off[0]), [(n, a, b)], off[1])

    def tup(*xs):
        return [x for x in xs if isinstance(x, tuple)]

    def raw(x):
        return x[0] if isinstance(x, tuple) else x

    def vcopy(o, i):
        emit("V", [lambda: g.vector.tensor_copy(out=o[0], in_=i[0])], [o], [i])

    def vtt(o, a, b, op):
        emit("V", [lambda: g.vector.tensor_tensor(out=o[0], in0=a[0], in1=b[0], op=op)], [o], [a, b])

    def vts(o, a, s1, s2, op0, op1=None):
        if op1 is None:
            f = lambda: g.vector.tensor_scalar(out=o[0], in0=a[0], scalar1=raw(s1), scalar2=None, op0=op0)
        else:
            f = lambda: g.vector.tensor_scalar(out=o[0], in0=a[0], scalar1=raw(s1), scalar2=raw(s2), op0=op0, op1=op1)
        emit("V", [f], [o], [a] + tup(s1, s2))

    def vscan(o, d0, d1, init, op0, op1):
        emit("V", [lambda: g.vector.tensor_tensor_scan(out=o[0], data0=d0[0], data1=d1[0], initial=init, op0=op0, op1=op1)],
             [o], [d0, d1])

    def vset(o, c):
        emit("V", [lambda: g.vector.memset(o[0], c)], [o], [])

    def vtr(o, i):
        emit("V", [lambda: g.vector.transpose(out=o[0], in_=i[0])], [o], [i])

    def vsum(o, i):
        emit("V", [lambda: g.vector.tensor_reduce(out=o[0], in_=i[0], axis=AxisListType.X, op=O.add)], [o], [i])

    def sact(o, i, func=AF.Copy, scale=1.0):
        emit("S", [lambda: g.scalar.activation(out=o[0], in_=i[0], func=func, scale=raw(scale))], [o], [i] + tup(scale))

    def mm(o, l, r, st, sp):
        return (lambda: g.tensor.matmul(o[0], l[0], r[0], st, sp)), o, l, r

    def pe(ms):
        emit("P", [m[0] for m in ms], [m[1] for m in ms], [x for m in ms for x in (m[2], m[3])])

    def load(q, sem, o, in_ap, tot):
        order(q, [], o[1])
        QUEUE[q].dma_start(out=o[0], in_=in_ap).then_inc(T.sem[sem], 16)
        total[sem] = 16 * tot
        record("D" + sem, [], o[1], sem, 16 * tot)

    def store(q, sem, out_ap, i):
        order(q, i[1], [])
        QUEUE[q].dma_start(out=out_ap, in_=i[0]).then_inc(T.sem[sem], 16)
        total[sem] = 16

    def lists(a, sem, src):
        for k in range(8):
            c = a + 16 * k
            load("Y", sem, (T.ml[0:64, c:c + 16], [("ml", c, c + 16)], []), src[k:k + 1, :], 8)

    def spread(sem, n, src):
        for f in range(16):
            load("Y", sem, (T[n][f:128:16, OWN:OWN + 1024], [(n + "_" + str(f), 0, 1)], []), src[:], 16)
        record("D" + sem, [], [(n, OWN, OWN + 1024)], sem, 256)
    load("S", "ld_b", R("bl", 0, 16), T.bx[:], 2)
    load("S", "ld_b", R("bl", 16, 32), T.bz[:], 2)
    lists(0, "ld_m", T.m)
    load("S", "ld_z", R("ZW", OWN, OWN + 1024), T.z[:], 1)
    load("Y", "ld_nz", R("tNZ", 0, 1024), T.nz[:], 1)
    lists(128, "ld_im", T.im)
    load("Y", "ld_nb", R("tNB", 0, 1024), T.nb[:], 1)

    def giota(o, pat, ch):
        emit("G", [lambda: g.iota(o[0], pat, 0, ch)], [o], [])

    def gsel(o, i, pat, base, ch):
        emit("G", [lambda: g.affine_select(o[0], i[0], pat, O.is_ge, 0.0, base, ch)], [o], [i])
    a128 = lambda n: R(n, 0, 128)
    a64 = lambda n: R(n, 0, 64)
    MP = R("pb6", 256, 384)
    vset(a128("onesf"), 1.0)
    giota(R("c_p", 0, 2), [[0, 2]], 1)
    giota(a128("c_it"), [[0, 8], [1, 16]], 0)
    gsel(a128("b1"), a128("onesf"), [[-16, 8], [0, 16]], 0, 1)
    gsel(a128("blkf"), a128("b1"), [[16, 8], [0, 16]], 15, -1)
    giota(R("c_c16", 0, 4), [[16, 4]], 0)
    vset(a64("ones64"), 1.0)
    vset(R("Es", 0, 144), 0.0)
    vset(a64("c25"), 0.25)
    vset(a64("c00"), 0.0)
    vts(R("fI", 0, 2), R("c_p", 0, 2), 15, None, O.bitwise_and)
    vcopy(a128("itf"), a128("c_it"))
    vcopy(R("ff", 0, 2), R("fI", 0, 2))
    vts(a128("reset"), a128("itf"), 0.0, None, O.is_gt)
    vts(a128("mask"), a128("itf"), C("ff"), None, O.is_equal)
    vts(C("f15"), C("ff"), -1.0, 15.0, O.mult, O.add)
    vscan(a64("thr"), a64("c25"), a64("c00"), 3.0 * 4.0 ** 33, O.mult, O.add)
    vtt(a128("identf"), a128("blkf"), a128("mask"), O.mult)
    vcopy(MP, a128("mask"))
    vts(R("Es", 15, 143, 16), R("blkf", 0, 128, 16), 16.0, None, O.mult)
    vts(a128("identn"), a128("identf"), -1.0, None, O.mult)
    vcopy(a128("identb"), a128("identf"))
    vcopy(R("BL", 0, 32), R("bl", 0, 32))
    vts(a128("biasd"), a128("identf"), C("f15"), None, O.mult)
    vts(R("q25", 0, 16), R("reset", 0, 16), 0.25, None, O.mult)
    vts(R("s0", 0, 16), R("reset", 0, 16), -1.0, 1.0, O.mult, O.add)
    vts(a64("mm1"), a64("mask"), -1.0, None, O.add)
    vscan(R("pwr", 0, 16), R("q25", 0, 16), R("s0", 0, 16), 0.0, O.mult, O.add)
    vtt(a64("t1"), a64("thr"), a64("mask"), O.mult)
    vtt(R("pm", 0, 16), R("pwr", 0, 16), R("mask", 0, 16), O.mult)
    vts(a64("nmB"), a64("mask"), -float(2 ** 24), float(2 ** 24), O.mult, O.add)
    vsum(C("pwc"), R("pm", 0, 16))
    vtt(a64("thrM"), a64("t1"), a64("mm1"), O.add)
    vcopy(R("c16f", 0, 4), R("c_c16", 0, 4))
    vts(R("lane4", 0, 4), R("c16f", 0, 4), C("ff"), None, O.add)
    for c in range(4):
        vts(R("W4", 128 * c, 128 * c + 128), a128("blkf"), C("pwc"), 4.0 ** (32 - 16 * c), O.mult, O.mult)
    vts(R("VL", 0, 4), R("lane4", 0, 4), 16.0, None, O.mult)
    sact(a128("blkp"), a128("blkf"), AF.Copy, 2.0)
    sact(a128("blkm"), a128("blkf"), AF.Copy, -2.0)
    sact(a128("blkV"), a128("blkf"), AF.Copy, -float(2 ** 20))
    sact(a128("idV"), a128("identf"), AF.Copy, -float(2 ** 20))
    sact(a128("idN"), a128("identf"), AF.Copy, float(2 ** 70))
    sact(a128("onesb"), a128("onesf"))

    def near(c):
        return topo.cores_of(c)

    def wmask(c, d):
        m = topo.mask(c, d)
        if d in near(c):
            for o in T.cores:
                if o not in near(c):
                    m &= ~topo.mask(c, o)
        return m

    def ones(m):
        return bin(m).count("1")

    def plan(s):
        ds = [(d, T.cores[(T.rank_of(s) - d) % N]) for d in (1, 2, 3)]
        rel = []
        for (d, t) in ds:
            twin = [(e, u) for (e, u) in ds if u != t and u in near(t)]
            if t not in near(s) and twin and topo.die(t) != topo.die(s):
                rel.append((twin[0][1], twin[0][0], t, d))
        far = [x[2] for x in rel]
        lead = [x[0] for x in rel]
        direct = [(d, t, t in lead) for (d, t) in ds if t not in far]
        return sorted(direct, key=lambda x: not x[2]), rel
    plans = {s: plan(s) for s in T.cores}
    duty = [(e, t, d) for s in T.cores for (u, e, t, d) in plans[s][1] if u == core]

    def targets(s):
        return [t for (d, t, l) in plans[s][0]] + [t for p in plans.values() for (u, e, t, d) in p[1] if u == s]
    writers = [s for s in T.cores if core in targets(s)]
    tell = len(set(targets(core)))
    come = []
    for s in T.cores:
        for (d, t, l) in plans[s][0]:
            if t == core:
                come.append(("b" if l else "a", d, ones(wmask(s, core))))
        for (u, e, t, d) in plans[s][1]:
            if t == core:
                come.append(("a", d, ones(wmask(u, core))))
    nsl = [0]
    block = lambda d: (OWN + 1024 + 256 * (d - 1), OWN + 1280 + 256 * (d - 1))

    def put(dst, win, d, src, sem):
        order("G", src[1], [])
        rid, pid = topo.addr(dst, core)
        a, b = block(d)
        m = wmask(core, dst)
        g.remote_dma(out_ap=T[win][:, a:b], in_ap=src[0], remote_sem=T.sem[sem], local_sem=T.sem.sl, pid=pid, routing_id=rid,
                     dma_engine_mask=m)
        nsl[0] += ones(m)

    Zown, Zall = ("ZW", OWN, OWN + 1024), ("ZW", OWN, OWN + 1792)
    Yown, Yall = ("YW", OWN, OWN + 1024), ("YW", OWN, OWN + 1792)

    def borders(e):
        vcopy(R("SY", 256 * e, 256 * e + 128), IND(*Yown, R("BL", 0, 8)))
        sact(R("SY", 256 * e + 128, 256 * e + 256), IND(*Yown, R("BL", 8, 16)))
        two = (("SZ", "ZW", "Z%d" % e), ("SY", "YW", "Y%d" % e))
        todo = [(w, x) for x in plans[core][0] for w in two]
        if e == 0:
            todo = [(w, x) for w in two for x in plans[core][0]]
        for (n, win, s), (d, t, l) in todo:
            put(t, win, d, R(n, 256 * e, 256 * e + 256), ("b" if l else "a") + s)
        for (n, win, s) in two:
            for k in "ab":
                v = sum(x[2] for x in come if x[0] == k)
                total[k + s] = v
                for x in come:
                    if x[0] == k:
                        record("A", [], [(win,) + block(x[1])], k + s, v)
            for (b, t, d) in duty:
                put(t, win, d, R(win, *block(b)), "a" + s)

    sact(R("SZ", 0, 256), IND(*Zown, R("BL", 16, 32)))
    mlp = lambda n, a: (T[n][0:64, a:a + 128], [(n, a, a + 128)], [])
    id64 = (T.identf[0:64, 0:64], [("identf", 0, 128)], [])

    def mlist(a, bank):
        vcopy(mlp("mlf", a), mlp("ml", a))
        o, i = R(bank, 0, 64), mlp("mlf", a)
        emit("P", [lambda: g.tensor.transpose(o[0], i[0], id64[0])], [o], [i, id64])
        vcopy(R("ML", a // 2, a // 2 + 64), o)
    mlist(0, "pb0")
    vcopy(R("YW", OWN, OWN + 512), IND(*Zown, R("ML", 0, 32)))
    sact(R("YW", OWN + 512, OWN + 1024), IND(*Zown, R("ML", 32, 64)))
    borders(0)
    need("Y", "aZ0", total["aZ0"])
    spread("ld_IM", "tIM", T.im)
    spread("ld_M", "tM", T.m)
    load("Y", "ld_x", R("tX", 0, 1024), T.x[:], 1)
    vcopy(R("tNZM", OWN, OWN + 1024), IND("tNZ", 0, 1024, R("ML", 0, 64)))
    mlist(128, "pb1")
    vcopy(R("L1", 64, 128), R("tNZM", OWN, OWN + 1024, 16))
    vcopy(R("L1", 0, 64), R("tNB", 0, 1024, 16))
    vcopy(R("tNBI", OWN, OWN + 1024), IND("tNB", 0, 1024, R("ML", 64, 128)))

    def step_lists():
        vcopy(a128("nf"), a128("L1"))
        vts(R("v5a", 0, 4), R("VL", 0, 4), 5.0, 1.0, O.mult, O.add)
        vts(R("v5b", 0, 4), R("v5a", 0, 4), 1023, None, O.bitwise_and)
        vcopy(R("V5", 0, 4), R("v5b", 0, 4))
    step_lists()

    for r in range(3):
        mt = "tM" if r == 0 else "MF"
        more = r < 2
        for (a, b) in CH:
            sact(R("Zt", 16 * a, 16 * b), IND(*Zall, R("L1", 64 + a, 64 + b)))
            b = min(b, 64 - YS)
            if a < b:
                vcopy(R("Yt", 16 * a, 16 * b), IND(*Yall, R("L1", a, b)))
        sact(R("Yt", 1024 - 16 * YS, 1024), IND(*Yall, R("L1", 64 - YS, 64)))
        for j, (a, b) in enumerate(CH):
            o = R("pb%d" % j, 0, 16 * (b - a))
            pe([mm(o, a128("identb"), R("Yt", 16 * a, 16 * b), True, False),
                mm(o, a128("identn"), R("Zt", 16 * a, 16 * b), False, True)])
        c0 = 16 * CH[0][1]
        vts(R("ng", 0, c0), R("pb0", 0, c0), -1.0, None, O.mult)
        vtt(R("AD", 0, c0), R("pb0", 0, c0), R("ng", 0, c0), O.max)
        for j in (1, 2):
            a, b = CH[j]
            sact(R("AD", 16 * a, 16 * b), R("pb%d" % j, 0, 16 * (b - a)), AF.Abs)
        K = R("pb3", 0, 64)
        pe([mm(K, a128("biasd"), a64("ones64"), True, False)] +
           [mm(K, R("Es", 15 - k, 143 - k), R("AD", k, 1024, 16), False, k == 15) for k in range(16)])
        OH = R("pb5", 0, 64)
        vtr(a64("KT"), K)
        vscan(a64("Fs"), a64("reset"), a64("KT"), 0.0, O.mult, O.max)
        for s in range(4):
            vts(R("OHt", 16 * s, 16 * s + 16), R("KT", 16 * s, 16 * s + 16), C("Fs", 16 * s + 15), None, O.is_equal)
        vtr(OH, a64("OHt"))
        vtt(R("pr", 0, 64), OH, R("nf", 0, 64), O.mult)
        vtt(R("pr", 64, 128), OH, R("nf", 64, 128), O.mult)
        ROW = R("pb4", 0, 128)
        pe([mm(ROW, a128("blkf"), a128("pr"), True, True)])
        vts(a64("kz"), K, 16.0, None, O.is_lt)
        vtt(a64("kz2"), a64("kz"), OH, O.mult)
        vtt(a128("mk"), ROW, a128("mask"), O.mult)
        vscan(a128("sc"), a128("reset"), a128("mk"), 0.0, O.mult, O.add)
        vts(R("LAQ", 0, 8), R("sc", 15, 128, 16), 1023.0, None, O.min)
        la, lq = R("LAQ", 0, 4), R("LAQ", 4, 8)
        vcopy(R("L2", 0, 64), IND("tNZM", OWN, OWN + 1024, la))
        vcopy(R("L2", 64, 128), IND("tNBI", OWN, OWN + 1024, lq))
        vcopy(R("L2", 128, 192), IND("tNZ", 0, 1024, lq))
        for n, c in (("Bt", 0), ("Bp", 128)):
            for h in (0, 1):
                sact(R(n, 512 * h, 512 * h + 512), IND(*Zall, R("L2", c + 32 * h, c + 32 * h + 32)))
        sact(R("At", 1024 - 16 * AS, 1024), IND(*Yall, R("L2", 128 - AS, 128)))
        vcopy(R("At", 0, 1024 - 16 * AS), IND(*Yall, R("L2", 64, 128 - AS)))
        vcopy(R("L2", 192, 256), IND("tNB", 0, 1024, la))
        vcopy(R("WP", 0, 64), IND("tIM", OWN, OWN + 1024, lq))
        vcopy(R("WP", 64, 128), IND(mt, OWN, OWN + 1024, la))
        vts(a128("gh"), ROW, 1024.0, None, O.is_ge)
        vtt(a128("mk2"), a128("WP"), MP, O.mult)
        sact(a128("AQ"), ROW)
        sact(R("NR", 0, 128, 2), R("AQ", 0, 64))
        sact(R("NR", 1, 128, 2), R("WP", 0, 64))
        vtt(R("T1", 0, 1024), IND(*Yall, R("L2", 192, 256)), R("Bt", 0, 1024), O.max)
        vscan(a128("sc2"), a128("reset"), a128("mk2"), 0.0, O.mult, O.add)
        vts(R("NLc", 0, 8), R("sc", 15, 128, 16), 1023.0, float(OWN), O.min, O.add)
        vts(R("NLc", 8, 16), R("sc2", 15, 128, 16), float(OWN), None, O.add)
        vcopy(R("LWP", 0, 8), R("sc2", 15, 128, 16))
        vtt(R("T2", 0, 1024), IND(*Yall, R("L2", 192, 256)), R("Bp", 0, 1024), O.max)
        if more:
            need("G", "cv", cnt["cv"])
            need("G", "cs", max(e[5] for w in ("ZW", "YW") for e in acc[w] if e[3] == "S"))
            need("G", "sl", nsl[0])
            for d in writers:
                rid, pid = topo.addr(d, core)
                g.remote_sem_update(T.sem["rdy%d" % (r + 1)], T.sem.sl, pid, rid, 1 << topo.engines(core, d)[0])
                nsl[0] += 1
            total["rdy%d" % (r + 1)] = tell
        Gn = R("pb6", 0, 64)
        dif = {}

        def diff(bk, src, h):
            a, b = 512 * h, 512 * h + 512
            o = R(bk, 0, 512)
            pe([mm(o, a128("identb"), R(src, a, b), True, False), mm(o, a128("identn"), R("At", a, b), False, True)])
            dif[src, h] = o

        def term(n, l):
            pe([mm(Gn, a128(l), R(n, k, 1024, 16), False, n == "R2" and k == 15) for k in range(16)])
        diff("pb0", "Bt", 0)
        diff("pb2", "Bp", 0)
        pe([mm(Gn, a128("idV"), R("gh", 0, 64), True, False), mm(Gn, a128("idV"), R("gh", 64, 128), False, False),
            mm(Gn, a128("blkV"), a64("kz2"), False, False)])
        term("T1", "blkp")
        diff("pb1", "Bt", 1)
        diff("pb5", "Bp", 1)
        for (n, src, h) in (("R1", "Bt", 0), ("R2", "Bp", 0), ("R1", "Bt", 1), ("R2", "Bp", 1)):
            o = R(n, 512 * h, 512 * h + 512)
            if n == "R1" and h == 0:
                vts(o, dif[src, h], 0.0, None, O.max)
            else:
                sact(o, dif[src, h], AF.Relu)
        term("T2", "blkm")
        term("R1", "blkm")
        term("R2", "blkp")
        sact(R("zz", 0, 64), IND(*Zown, lq))
        sact(R("xx", 0, 64), IND("tX", 0, 1024, la))
        sact(R("zz", 64, 128), IND(*Zown, R("LWP", 4, 8)))
        sact(R("xx", 64, 128), IND("tX", 0, 1024, R("LWP", 0, 4)))
        eqs, at = [], 0
        for c in range(4):
            for col in (C("sc", 16 * c + 15), C("sc2", 16 * c + 15)):
                w = 128 - 32 * c
                vts(R("EQ", at, at + w), R("NR", 32 * c, 128), col, None, O.is_equal)
                eqs.append((c, at, w))
                at += w
        vtt(a64("x1"), Gn, a64("TH") if r else a64("nmB"), O.is_gt)
        vscan(a64("sp"), a64("reset"), a64("x1"), 0.0, O.mult, O.add)
        for c in range(4):
            vts(R("WT", 128 * c, 128 * c + 128), R("W4", 128 * c, 128 * c + 128), C("sp", 16 * c + 15), None, O.mult)
        vts(a64("npr"), Gn, C("thc") if r else 0.0, None, O.is_le)
        xz = R("pb4", 128, 256)
        pe([mm(xz, a128("identb"), a128("xx"), True, False), mm(xz, a128("identn"), a128("zz"), False, True)])
        vts(a128("cl"), xz, -1.0, 1.0, O.max, O.min)
        CS = R("pb7", 0, 64)
        for c in range(4):
            pe([mm(R("pb7", 16 * c, 64), R("WT", 128 * c, 128 * c + 128), R("EQ", at + nm, at + w, 2),
                   c == 0 and (at, nm) == (0, 0), False) for (c2, at, w) in eqs if c2 == c for nm in (0, 1)])
        pe([mm(CS, a128("idN"), a64("npr"), False, True)])
        nzp = R("pb3", 128, 256)
        pe([mm(nzp, a128("identb"), a128("zz"), True, False), mm(nzp, a128("identb"), a128("cl"), False, True)])
        sact(a128("nzv"), nzp)
        if more:
            vts(R("oq", 0, 4), R("sc", 79, 128, 16), 1024.0, None, O.is_lt)
            vtt(R("d1", 0, 4), R("sc2", 15, 64, 16), R("V5", 0, 4), O.subtract)
            vtt(R("d2", 0, 4), R("d1", 0, 4), R("oq", 0, 4), O.mult)
            vtt(R("alt", 0, 4), R("d2", 0, 4), R("V5", 0, 4), O.add)
            vtt(R("da", 0, 4), R("sc", 15, 64, 16), R("alt", 0, 4), O.subtract)
        vtt(a64("cm"), CS, a64("thrM"), O.is_le)
        vscan(a64("cl2"), a64("reset"), a64("cm"), 0.0, O.mult, O.add)
        for c in range(4):
            vts(R("OFF", c, 16, 4), R("NLc", c, 16, 4), C("cl2", 16 * c + 15), C("lane4", c), O.mult, O.max)
        oa, oqq, ow, op = [R("OFF", 4 * n, 4 * n + 4) for n in range(4)]
        sca = lambda n, off, d: vcopy(IND(n, 0, OWN + 1024, off), d)
        sca("ZW", oqq, R("nzv", 0, 64))
        sca("ZW", op, R("nzv", 64, 128))
        if not more:
            store("Y", "st_z", T.zo[:], R("ZW", OWN, OWN + 1024))
            sca("MF", oa, R("AQ", 64, 128))
            sca("MF", ow, R("WP", 64, 128))
            store("Y", "st_m", T.mo[:], (T.MF[0:128:16, OWN:OWN + 1024], [("MF", OWN, OWN + 1024)], []))
            break
        e = r + 1
        sact(R("SZ", 256 * e, 256 * e + 256), IND(*Zown, R("BL", 16, 32)))
        sca("YW", oa, R("nzv", 0, 64))
        sca("YW", ow, R("nzv", 64, 128))
        need("G", "rdy%d" % e, tell)
        borders(e)
        vtt(R("d3", 0, 4), R("da", 0, 4), R("cl2", 15, 64, 16), O.mult)
        sca("tNZM", oa, R("L2", 128, 192))
        sca("tNZM", ow, R("L2", 0, 64))
        vtt(R("VL", 0, 4), R("d3", 0, 4), R("alt", 0, 4), O.add)
        vsum(C("cn"), a64("cm"))
        vcopy(R("vl", 0, 4), R("VL", 0, 4))
        vcopy(C("cnt"), C("cn"))
        vcopy(R("L1", 0, 64), IND("tNB", 0, 1024, R("vl", 0, 4)))
        pe([mm(R("pb7", 256, 257), a128("onesb"), C("cnt"), True, True)])
        vcopy(R("L1", 64, 128), IND("tNZM", OWN, OWN + 1024, R("vl", 0, 4)))
        sca("tNBI", oqq, R("L2", 192, 256))
        sca("tNBI", op, R("L2", 64, 128))
        vcopy(C("thi"), R("pb7", 256, 257))
        step_lists()
        vts(C("thj"), C("thi"), 31, None, O.bitwise_and)
        sca(mt, oa, R("AQ", 64, 128))
        vcopy(C("thc"), C("thj"))
        sca(mt, ow, R("WP", 64, 128))
        vts(a64("TH"), a64("nmB"), C("thc"), None, O.add)
        sca("tIM", oqq, R("AQ", 0, 64))
        sca("tIM", op, R("WP", 0, 64))
        if r == 0:
            vcopy(R("MF", OWN, OWN + 1024), R("tM", OWN, OWN + 1024))

    total.update(cnt)
    total["sl"] = nsl[0]
    for s, v in total.items():
        if max(seen[q].get(s, 0) for q in seen) < v:
            g.wait_ge(T.sem[s], v)
